import numpy as np
import ml_dtypes


def mxq(x, axis, fmt="e4m3"):
    dtype, down = {"e4m3": (ml_dtypes.float8_e4m3fn, 7), "e5m2": (ml_dtypes.float8_e5m2, 14)}[fmt]
    v = np.moveaxis(np.asarray(x, np.float32).astype(ml_dtypes.bfloat16).astype(np.float64), axis, -1)
    blocks = v.reshape(v.shape[:-1] + (-1, 32))
    amax = np.abs(blocks).max(-1, keepdims=True)
    byte = np.maximum(np.where(amax > 0, np.frexp(amax)[1] - 1 + 127, 0) - down, 1)
    scale = np.exp2(byte - 127.0)
    codes = (blocks / scale).astype(np.float32).astype(dtype).astype(np.float64)
    return np.moveaxis((codes * scale).reshape(v.shape), -1, axis)


WIDE = False


def mx_kscale(k):
    if not WIDE:
        return np.ones(k)
    levels = np.array([10, -10, 5, -5, 0])
    if k % 512:
        return np.exp2(np.random.permutation(np.resize(levels, k // 32))).repeat(32)
    a = np.empty((k // 512, 16))
    for p in range(k // 512):
        a[p, :8] = np.random.permutation(np.resize(levels, 8))
        for g in range(8):
            far = levels[np.abs(levels - a[p, g]) >= 10]
            a[p, g + 8] = far[np.random.randint(len(far))]
    return np.exp2(a.ravel()).repeat(32)


def f64(x):
    return np.asarray(x).astype(np.float64)


def striped(idx):
    return np.tile(idx.reshape(-1, 16).T, (8, 1)).astype(np.uint16)


def unstriped(offs):
    return offs[:16].T.reshape(-1).astype(np.int64)


def pack_weight(w):
    k, n = w.shape
    w = f64(np.asarray(w, np.float32).astype(ml_dtypes.bfloat16)).reshape(k // 32, 32, n)
    amax = np.abs(w).max(1)
    byte = np.clip(np.where(amax > 0, np.frexp(amax)[1] - 1 + 127 - 7, 1), 1, 254)
    scaled = (w * np.exp2(127.0 - byte)[:, None, :]).reshape(k, n).astype(np.float32)
    words = np.ascontiguousarray(scaled.reshape(k // 512, 128, 4, n).transpose(0, 1, 3, 2)).astype(ml_dtypes.float8_e4m3fn).view(np.uint8)
    return words, np.ascontiguousarray(byte.astype(np.uint8).reshape(k // 512, 16, n))


def unpack_weight(words, scales):
    g, p, n, _ = words.shape
    vals = np.ascontiguousarray(words).view(ml_dtypes.float8_e4m3fn).astype(np.float64) * np.repeat(np.exp2(scales.astype(np.float64) - 127.0), 8, axis=1)[..., None]
    return vals.transpose(0, 1, 3, 2).reshape(g * 512, n)


def relu(v):
    return np.maximum(v, 0.0)


K, T, S, V, H, N = 512, 1024, 512, 256, 512, 128


def setup_inputs():
    n = np.random.standard_normal
    s = mx_kscale(K)[:, None]
    u = mx_kscale(H)
    packed_xT = pack_weight(n((K, T)) * s)
    return {
        "x_words": packed_xT[0],
        "x_scales": packed_xT[1],
        "w1": (n((K, H)) / np.sqrt(K) / s * u).astype(np.float32),
        "w2": (n((H, N)) / np.sqrt(2 * H) / u[:, None]).astype(np.float32),
        "w3": (n((H, N)) / np.sqrt(2 * H) / u[:, None]).astype(np.float32),
        "offs": striped(np.random.permutation(T)[:S]),
    }


def reference(x_words, x_scales, w1, w2, w3, offs):
    xq = unpack_weight(x_words, x_scales)[:, unstriped(offs)]
    h = relu(mxq(f64(w1), 0, "e4m3").T @ xq)
    low = 0.5 * (h[:, :V] + h[:, V:2 * V])
    high = 0.5 * (h[:, :V] - h[:, V:2 * V])
    return mxq(f64(w2), 0, "e4m3").T @ mxq(low, 0, "e4m3") + mxq(f64(w3), 0, "e4m3").T @ mxq(high, 0, "e4m3")

@@ -1,0 +1,153 @@
+from contextlib import ExitStack
+
+import concourse.mybir as mybir
+
+K, T, S, V, H, N = 512, 1024, 512, 256, 512, 128
+FLOPS = 2 * K * H * S + 2 * 2 * H * N * V
+
+F32 = mybir.dt.float32
+BF16 = mybir.dt.bfloat16
+I32 = mybir.dt.int32
+U32 = mybir.dt.uint32
+U16 = mybir.dt.uint16
+U8 = mybir.dt.uint8
+FP8X4 = mybir.dt.float8_e4m3fn_x4
+ALU = mybir.AluOpType
+ACT = mybir.ActivationFunctionType
+
+P = 128
+PACK = 4
+HALVES = 2
+HALF_COLS = H // HALVES
+HALF_M = HALF_COLS // PACK
+CHUNK = 128
+CHUNKS = V // CHUNK
+LIST_ROWS = 16
+
+
+def tile_picked_haar_relu_p_kernel(tc, x_words, x_scales, w1, w2, w3, offs, out):
+    nc = tc.nc
+    with ExitStack() as ctx:
+        keep = ctx.enter_context(tc.tile_pool(name="keep", bufs=1))
+        stage = ctx.enter_context(tc.tile_pool(name="stage", bufs=2))
+        psum = ctx.enter_context(tc.psum_pool(name="psum", bufs=1))
+
+        offsets = keep.tile([P, S // LIST_ROWS], U16, name="offsets")
+        nc.sync.dma_start(offsets[:], offs)
+
+        byte_table = keep.tile([P, T], U8, name="byte_table", tag="w1_grouped01", align_bytes=64)
+        nc.vector.memset(byte_table[:].bitcast(I32), 0)
+        for q in range(4):
+            nc.scalar.dma_start(byte_table[32 * q : 32 * q + 4, :].bitcast(I32), x_scales[0, 4 * q : 4 * q + 4, :].bitcast(I32))
+
+        w1_rows = w1.rearrange("(p j) c -> p j c", j=PACK)
+        w1_raw = []
+        for h in range(HALVES):
+            raw = stage.tile([P, PACK, HALF_COLS], F32, name="raw", tag="raw")
+            nc.sync.dma_start(raw[:], w1_rows[:, :, h * HALF_COLS : (h + 1) * HALF_COLS])
+            w1_raw.append(raw)
+
+        word_table = keep.tile([P, T], U32, name="word_table", align_bytes=64)
+        nc.sync.dma_start(word_table[:].bitcast(I32), x_words[0].rearrange("p n t -> p (n t)").bitcast(I32))
+
+        x_bytes = keep.tile([P, S], U8, name="x_bytes", align_bytes=64)
+        nc.vector.tensor_copy(x_bytes[:], byte_table[:].indirect(offsets[:]))
+
+        w1_codes = [keep.tile([P, P], U32, name=f"w1_codes{t}", align_bytes=64) for t in range(PACK)]
+        w1_bytes = [keep.tile([P, P], U8, name=f"w1_bytes{t}", align_bytes=64) for t in range(PACK)]
+        for h in range(HALVES):
+            src = w1_raw[h][:].rearrange("p j (m t) -> p m t j", t=PACK)
+            shares = []
+            for e in range(2):
+                grouped = keep.tile([P, 2, HALF_M, PACK], BF16, name=f"w1_grouped{h}{e}", tag=f"w1_grouped{h}{e}", align_bytes=64)
+                dst = grouped[:].rearrange("p t m j -> p m t j")
+                if e == 0:
+                    nc.scalar.copy(dst, src[:, :, 0:2, :])
+                else:
+                    nc.vector.tensor_copy(dst, src[:, :, 2:4, :])
+                shares.append(grouped)
+            cols = slice(h * HALF_M, (h + 1) * HALF_M)
+            for t in (2, 3, 0, 1):
+                nc.vector.quantize_mx(
+                    out=w1_codes[t][:, cols].bitcast(FP8X4),
+                    scales=w1_bytes[t][:, cols],
+                    in_=shares[t // 2][:, t % 2, :, :].rearrange("p m j -> p (m j)"),
+                )
+
+        w23_raw = stage.tile([P, 2, PACK, N], F32, name="w23_raw", tag="raw")
+        for i, w in enumerate((w2, w3)):
+            nc.sync.dma_start(w23_raw[:, i, :, :], w.rearrange("(p j) n -> p j n", j=PACK))
+
+        def first_product(first, name):
+            words = keep.tile([P, CHUNK], U32, name=f"x_words_{name}", align_bytes=64)
+            nc.vector.tensor_copy(words[:], word_table[:].indirect(offsets[:, first // LIST_ROWS : (first + CHUNK) // LIST_ROWS]))
+            bank = psum.tile([P, PACK, CHUNK], F32, name=f"bank_{name}")
+            for t in range(PACK):
+                nc.tensor.matmul_mx(
+                    out=bank[:, t, :],
+                    lhsT=w1_codes[t][:].bitcast(FP8X4),
+                    lhsT_scale=w1_bytes[t][:],
+                    rhs=words[:].bitcast(FP8X4),
+                    rhs_scale=x_bytes[:, first : first + CHUNK],
+                    start=True,
+                    stop=True,
+                )
+            return bank[:].rearrange("p t v -> p v t")
+
+        banks = []
+        for c in range(CHUNKS):
+            second = first_product(V + c * CHUNK, f"b{c}")
+            banks.append((first_product(c * CHUNK, f"a{c}"), second))
+
+        w23_grouped = keep.tile([P, 2, N, PACK], BF16, name="w23_grouped", align_bytes=64)
+        w23_codes = keep.tile([P, 2 * N], U32, name="w23_codes", align_bytes=64)
+        w23_bytes = keep.tile([P, 2 * N], U8, name="w23_bytes", align_bytes=64)
+
+        def relu_second(c):
+            relu_b = keep.tile([P, CHUNK, PACK], F32, name=f"relu_b{c}")
+            nc.scalar.activation(relu_b[:], banks[c][1], ACT.Relu)
+            nc.scalar.copy(
+                w23_grouped[:, c, :, :].rearrange("p (n i) j -> p n j i", i=4),
+                w23_raw[:, c, :, :].rearrange("p j (n i) -> p n j i", i=4),
+            )
+            return relu_b
+
+        def band(c, relu_b, name, op):
+            values = keep.tile([P, CHUNK, PACK], BF16, name=f"{name}{c}", align_bytes=64)
+            nc.vector.scalar_tensor_tensor(values[:], banks[c][0], 0.0, relu_b[:], ALU.max, op)
+            return values
+
+        def quantized(values, name):
+            codes = keep.tile([P, CHUNK], U32, name=f"{name}_codes", align_bytes=64)
+            scales = keep.tile([P, CHUNK], U8, name=f"{name}_bytes", align_bytes=64)
+            nc.vector.quantize_mx(out=codes[:].bitcast(FP8X4), scales=scales[:], in_=values[:].rearrange("p v t -> p (v t)"))
+            return codes, scales
+
+        def second_product(c, operands):
+            acc = psum.tile([P, CHUNK], F32, name=f"acc{c}")
+            for i, (codes, scales) in enumerate(operands):
+                nc.tensor.matmul_mx(
+                    out=acc[:],
+                    lhsT=w23_codes[:, i * N : (i + 1) * N].bitcast(FP8X4),
+                    lhsT_scale=w23_bytes[:, i * N : (i + 1) * N],
+                    rhs=codes[:].bitcast(FP8X4),
+                    rhs_scale=scales[:],
+                    start=(i == 0),
+                    stop=(i == 1),
+                )
+            result = keep.tile([P, CHUNK], F32, name=f"result{c}")
+            nc.scalar.activation(result[:], acc[:], ACT.Copy, scale=0.5)
+            nc.sync.dma_start(out[:, c * CHUNK : (c + 1) * CHUNK], result[:])
+
+        relu_b0 = relu_second(0)
+        low0 = band(0, relu_b0, "low", ALU.add)
+        high0 = band(0, relu_b0, "high", ALU.subtract)
+        operands0 = [quantized(low0, "low0"), quantized(high0, "high0")]
+        relu_b1 = relu_second(1)
+        low1 = band(1, relu_b1, "low", ALU.add)
+        nc.vector.quantize_mx(
+            out=w23_codes[:].bitcast(FP8X4), scales=w23_bytes[:], in_=w23_grouped[:].rearrange("p i n j -> p (i n j)")
+        )
+        second_product(0, operands0)
+        high1 = band(1, relu_b1, "high", ALU.subtract)
+        second_product(1, [quantized(low1, "low1"), quantized(high1, "high1")])

@@ -29,65 +29,65 @@ def tile_picked_haar_relu_p_kernel(tc, x_words, x_scales, w1, w2, w3, offs, out)
     nc = tc.nc
     with ExitStack() as ctx:
         keep = ctx.enter_context(tc.tile_pool(name="keep", bufs=1))
-        stage = ctx.enter_context(tc.tile_pool(name="stage", bufs=2))
+        reuse = ctx.enter_context(tc.tile_pool(name="reuse", bufs=1))
         psum = ctx.enter_context(tc.psum_pool(name="psum", bufs=1))
 
         offsets = keep.tile([P, S // LIST_ROWS], U16, name="offsets")
         nc.sync.dma_start(offsets[:], offs)
 
-        byte_table = keep.tile([P, T], U8, name="byte_table", tag="w1_grouped01", align_bytes=64)
+        scale_rows = keep.tile([P, T], U8, name="scale_rows")
+        byte_table = keep.tile([P, T], U8, name="byte_table", align_bytes=64)
         nc.vector.memset(byte_table[:].bitcast(I32), 0)
         for q in range(4):
-            nc.scalar.dma_start(byte_table[32 * q : 32 * q + 4, :].bitcast(I32), x_scales[0, 4 * q : 4 * q + 4, :].bitcast(I32))
+            rows = slice(32 * q, 32 * q + 4)
+            queue = nc.scalar if q < 2 else nc.sync
+            queue.dma_start(scale_rows[rows, :].bitcast(I32), x_scales[0, 4 * q : 4 * q + 4, :].bitcast(I32))
+            nc.vector.tensor_copy(byte_table[rows, :].bitcast(I32), scale_rows[rows, :].bitcast(I32))
 
         w1_rows = w1.rearrange("(p j) c -> p j c", j=PACK)
-        w1_raw = []
-        for h in range(HALVES):
-            raw = stage.tile([P, PACK, HALF_COLS], F32, name="raw", tag="raw")
-            nc.sync.dma_start(raw[:], w1_rows[:, :, h * HALF_COLS : (h + 1) * HALF_COLS])
-            w1_raw.append(raw)
-
+        w1_raw = [keep.tile([P, PACK, HALF_COLS], F32, name=f"w1_raw{h}") for h in range(HALVES)]
+        nc.sync.dma_start(w1_raw[0][:], w1_rows[:, :, 0:HALF_COLS])
+        nc.sync.dma_start(w1_raw[1][:], w1_rows[:, :, HALF_COLS:H])
         word_table = keep.tile([P, T], U32, name="word_table", align_bytes=64)
         nc.sync.dma_start(word_table[:].bitcast(I32), x_words[0].rearrange("p n t -> p (n t)").bitcast(I32))
+        w23_raw = [keep.tile([P, PACK, N], F32, name=f"w23_raw{i}") for i in range(2)]
+        for i, w in enumerate((w2, w3)):
+            nc.sync.dma_start(w23_raw[i][:], w.rearrange("(p j) n -> p j n", j=PACK))
 
         x_bytes = keep.tile([P, S], U8, name="x_bytes", align_bytes=64)
         nc.vector.tensor_copy(x_bytes[:], byte_table[:].indirect(offsets[:]))
 
-        w1_codes = [keep.tile([P, P], U32, name=f"w1_codes{t}", align_bytes=64) for t in range(PACK)]
-        w1_bytes = [keep.tile([P, P], U8, name=f"w1_bytes{t}", align_bytes=64) for t in range(PACK)]
-        for h in range(HALVES):
-            src = w1_raw[h][:].rearrange("p j (m t) -> p m t j", t=PACK)
-            shares = []
-            for e in range(2):
-                grouped = keep.tile([P, 2, HALF_M, PACK], BF16, name=f"w1_grouped{h}{e}", tag=f"w1_grouped{h}{e}", align_bytes=64)
-                dst = grouped[:].rearrange("p t m j -> p m t j")
-                if e == 0:
-                    nc.scalar.copy(dst, src[:, :, 0:2, :])
-                else:
-                    nc.vector.tensor_copy(dst, src[:, :, 2:4, :])
-                shares.append(grouped)
-            cols = slice(h * HALF_M, (h + 1) * HALF_M)
-            for t in (2, 3, 0, 1):
-                nc.vector.quantize_mx(
-                    out=w1_codes[t][:, cols].bitcast(FP8X4),
-                    scales=w1_bytes[t][:, cols],
-                    in_=shares[t // 2][:, t % 2, :, :].rearrange("p m j -> p (m j)"),
-                )
+        def quantized(values, width, name):
+            codes = keep.tile([P, width], U32, name=f"{name}_codes", align_bytes=64)
+            scales = keep.tile([P, width], U8, name=f"{name}_bytes", align_bytes=64)
+            nc.vector.quantize_mx(out=codes[:].bitcast(FP8X4), scales=scales[:], in_=values)
+            return codes, scales
 
-        w23_raw = stage.tile([P, 2, PACK, N], F32, name="w23_raw", tag="raw")
-        for i, w in enumerate((w2, w3)):
-            nc.sync.dma_start(w23_raw[:, i, :, :], w.rearrange("(p j) n -> p j n", j=PACK))
+        w1_q = {}
+        grouped = {}
+        for first_slot, copy in ((2, nc.vector.tensor_copy), (0, nc.scalar.copy)):
+            grouped[first_slot] = reuse.tile([P, 2, P, PACK], BF16, name=f"w1_grouped{first_slot}", tag=f"slots{first_slot}", align_bytes=64)
+            for h in range(HALVES):
+                src = w1_raw[h][:].rearrange("p j (m t) -> p m t j", t=PACK)
+                dst = grouped[first_slot][:, :, h * HALF_M : (h + 1) * HALF_M, :].rearrange("p t m j -> p m t j")
+                copy(dst, src[:, :, first_slot : first_slot + 2, :])
+        for first_slot in (2, 0):
+            codes, scales = quantized(grouped[first_slot][:].rearrange("p t m j -> p (t m j)"), 2 * P, f"w1_{first_slot}")
+            for i in range(2):
+                w1_q[first_slot + i] = (codes[:, i * P : (i + 1) * P], scales[:, i * P : (i + 1) * P])
+
+        picked_words = reuse.tile([P, S], U32, name="picked_words", tag="slots0", align_bytes=64)
 
         def first_product(first, name):
-            words = keep.tile([P, CHUNK], U32, name=f"x_words_{name}", align_bytes=64)
-            nc.vector.tensor_copy(words[:], word_table[:].indirect(offsets[:, first // LIST_ROWS : (first + CHUNK) // LIST_ROWS]))
+            words = picked_words[:, first : first + CHUNK]
+            nc.vector.tensor_copy(words, word_table[:].indirect(offsets[:, first // LIST_ROWS : (first + CHUNK) // LIST_ROWS]))
             bank = psum.tile([P, PACK, CHUNK], F32, name=f"bank_{name}")
-            for t in range(PACK):
+            for t in (2, 3, 0, 1):
                 nc.tensor.matmul_mx(
                     out=bank[:, t, :],
-                    lhsT=w1_codes[t][:].bitcast(FP8X4),
-                    lhsT_scale=w1_bytes[t][:],
-                    rhs=words[:].bitcast(FP8X4),
+                    lhsT=w1_q[t][0].bitcast(FP8X4),
+                    lhsT_scale=w1_q[t][1],
+                    rhs=words.bitcast(FP8X4),
                     rhs_scale=x_bytes[:, first : first + CHUNK],
                     start=True,
                     stop=True,
@@ -99,37 +99,28 @@ def tile_picked_haar_relu_p_kernel(tc, x_words, x_scales, w1, w2, w3, offs, out)
             second = first_product(V + c * CHUNK, f"b{c}")
             banks.append((first_product(c * CHUNK, f"a{c}"), second))
 
-        w23_grouped = keep.tile([P, 2, N, PACK], BF16, name="w23_grouped", align_bytes=64)
-        w23_codes = keep.tile([P, 2 * N], U32, name="w23_codes", align_bytes=64)
-        w23_bytes = keep.tile([P, 2 * N], U8, name="w23_bytes", align_bytes=64)
+        w23_grouped = []
+        for i, copy in enumerate((nc.scalar.copy, nc.vector.tensor_copy)):
+            values = keep.tile([P, N, PACK], BF16, name=f"w23_grouped{i}", align_bytes=64)
+            copy(values[:].rearrange("p (n i) j -> p n j i", i=4), w23_raw[i][:].rearrange("p j (n i) -> p n j i", i=4))
+            w23_grouped.append(values)
+        w23_q = [quantized(values[:].rearrange("p n j -> p (n j)"), N, f"w23_{i}") for i, values in enumerate(w23_grouped)]
 
-        def relu_second(c):
+        for c in range(CHUNKS):
             relu_b = keep.tile([P, CHUNK, PACK], F32, name=f"relu_b{c}")
             nc.scalar.activation(relu_b[:], banks[c][1], ACT.Relu)
-            nc.scalar.copy(
-                w23_grouped[:, c, :, :].rearrange("p (n i) j -> p n j i", i=4),
-                w23_raw[:, c, :, :].rearrange("p j (n i) -> p n j i", i=4),
-            )
-            return relu_b
-
-        def band(c, relu_b, name, op):
-            values = keep.tile([P, CHUNK, PACK], BF16, name=f"{name}{c}", align_bytes=64)
-            nc.vector.scalar_tensor_tensor(values[:], banks[c][0], 0.0, relu_b[:], ALU.max, op)
-            return values
-
-        def quantized(values, name):
-            codes = keep.tile([P, CHUNK], U32, name=f"{name}_codes", align_bytes=64)
-            scales = keep.tile([P, CHUNK], U8, name=f"{name}_bytes", align_bytes=64)
-            nc.vector.quantize_mx(out=codes[:].bitcast(FP8X4), scales=scales[:], in_=values[:].rearrange("p v t -> p (v t)"))
-            return codes, scales
-
-        def second_product(c, operands):
+            bands = []
+            for name, op in (("low", ALU.add), ("high", ALU.subtract)):
+                values = keep.tile([P, CHUNK, PACK], BF16, name=f"{name}{c}", align_bytes=64)
+                nc.vector.scalar_tensor_tensor(values[:], banks[c][0], 0.0, relu_b[:], ALU.max, op)
+                bands.append(values)
             acc = psum.tile([P, CHUNK], F32, name=f"acc{c}")
-            for i, (codes, scales) in enumerate(operands):
+            for i, values in enumerate(bands):
+                codes, scales = quantized(values[:].rearrange("p v t -> p (v t)"), CHUNK, f"band{c}{i}")
                 nc.tensor.matmul_mx(
                     out=acc[:],
-                    lhsT=w23_codes[:, i * N : (i + 1) * N].bitcast(FP8X4),
-                    lhsT_scale=w23_bytes[:, i * N : (i + 1) * N],
+                    lhsT=w23_q[i][0][:].bitcast(FP8X4),
+                    lhsT_scale=w23_q[i][1][:],
                     rhs=codes[:].bitcast(FP8X4),
                     rhs_scale=scales[:],
                     start=(i == 0),
@@ -138,16 +129,3 @@ def tile_picked_haar_relu_p_kernel(tc, x_words, x_scales, w1, w2, w3, offs, out)
             result = keep.tile([P, CHUNK], F32, name=f"result{c}")
             nc.scalar.activation(result[:], acc[:], ACT.Copy, scale=0.5)
             nc.sync.dma_start(out[:, c * CHUNK : (c + 1) * CHUNK], result[:])
-
-        relu_b0 = relu_second(0)
-        low0 = band(0, relu_b0, "low", ALU.add)
-        high0 = band(0, relu_b0, "high", ALU.subtract)
-        operands0 = [quantized(low0, "low0"), quantized(high0, "high0")]
-        relu_b1 = relu_second(1)
-        low1 = band(1, relu_b1, "low", ALU.add)
-        nc.vector.quantize_mx(
-            out=w23_codes[:].bitcast(FP8X4), scales=w23_bytes[:], in_=w23_grouped[:].rearrange("p i n j -> p (i n j)")
-        )
-        second_product(0, operands0)
-        high1 = band(1, relu_b1, "high", ALU.subtract)
-        second_product(1, [quantized(low1, "low1"), quantized(high1, "high1")])

@@ -64,22 +64,31 @@ def tile_picked_haar_relu_p_kernel(tc, x_words, x_scales, w1, w2, w3, offs, out)
             return codes, scales
 
         w1_q = {}
-        grouped = {}
-        for first_slot, copy in ((2, nc.vector.tensor_copy), (0, nc.scalar.copy)):
-            grouped[first_slot] = reuse.tile([P, 2, P, PACK], BF16, name=f"w1_grouped{first_slot}", tag=f"slots{first_slot}", align_bytes=64)
-            for h in range(HALVES):
-                src = w1_raw[h][:].rearrange("p j (m t) -> p m t j", t=PACK)
-                dst = grouped[first_slot][:, :, h * HALF_M : (h + 1) * HALF_M, :].rearrange("p t m j -> p m t j")
-                copy(dst, src[:, :, first_slot : first_slot + 2, :])
+        grouped = {
+            slot: reuse.tile([P, 2, P, PACK], BF16, name=f"w1_grouped{slot}", tag=f"slots{slot}", align_bytes=64) for slot in (0, 2)
+        }
+
+        def deal_w1(copy, h, slot, m0, m1):
+            src = w1_raw[h][:].rearrange("p j (m t) -> p m t j", t=PACK)
+            dst = grouped[slot][:, :, h * HALF_M + m0 : h * HALF_M + m1, :].rearrange("p t m j -> p m t j")
+            copy(dst, src[:, m0:m1, slot : slot + 2, :])
+
+        deal_w1(nc.scalar.copy, 0, 0, 0, HALF_M)
+        deal_w1(nc.scalar.copy, 0, 2, 0, HALF_M // 2)
+        deal_w1(nc.vector.tensor_copy, 0, 2, HALF_M // 2, HALF_M)
+        deal_w1(nc.vector.tensor_copy, 1, 2, 0, HALF_M)
+        deal_w1(nc.scalar.copy, 1, 0, 0, HALF_M)
         for first_slot in (2, 0):
             codes, scales = quantized(grouped[first_slot][:].rearrange("p t m j -> p (t m j)"), 2 * P, f"w1_{first_slot}")
             for i in range(2):
                 w1_q[first_slot + i] = (codes[:, i * P : (i + 1) * P], scales[:, i * P : (i + 1) * P])
 
-        picked_words = reuse.tile([P, S], U32, name="picked_words", tag="slots0", align_bytes=64)
+        words_first = reuse.tile([P, CHUNK], U32, name="words_first", tag="slots2", align_bytes=64)
+        words_rest = reuse.tile([P, 3 * CHUNK], U32, name="words_rest", tag="slots0", align_bytes=64)
+        places = {"b0": words_first[:], "a0": words_rest[:, 0:CHUNK], "b1": words_rest[:, CHUNK : 2 * CHUNK], "a1": words_rest[:, 2 * CHUNK :]}
 
         def first_product(first, name):
-            words = picked_words[:, first : first + CHUNK]
+            words = places[name]
             nc.vector.tensor_copy(words, word_table[:].indirect(offsets[:, first // LIST_ROWS : (first + CHUNK) // LIST_ROWS]))
             bank = psum.tile([P, PACK, CHUNK], F32, name=f"bank_{name}")
             for t in (2, 3, 0, 1):
@@ -99,33 +108,40 @@ def tile_picked_haar_relu_p_kernel(tc, x_words, x_scales, w1, w2, w3, offs, out)
             second = first_product(V + c * CHUNK, f"b{c}")
             banks.append((first_product(c * CHUNK, f"a{c}"), second))
 
-        w23_grouped = []
-        for i, copy in enumerate((nc.scalar.copy, nc.vector.tensor_copy)):
-            values = keep.tile([P, N, PACK], BF16, name=f"w23_grouped{i}", align_bytes=64)
-            copy(values[:].rearrange("p (n i) j -> p n j i", i=4), w23_raw[i][:].rearrange("p j (n i) -> p n j i", i=4))
-            w23_grouped.append(values)
-        w23_q = [quantized(values[:].rearrange("p n j -> p (n j)"), N, f"w23_{i}") for i, values in enumerate(w23_grouped)]
+        w23_grouped = keep.tile([P, 2, N, PACK], BF16, name="w23_grouped", align_bytes=64)
+        for i in range(2):
+            nc.scalar.copy(
+                w23_grouped[:, i, :, :].rearrange("p (n i) j -> p n j i", i=4),
+                w23_raw[i][:].rearrange("p j (n i) -> p n j i", i=4),
+            )
+        w23_codes, w23_bytes = quantized(w23_grouped[:].rearrange("p i n j -> p (i n j)"), 2 * N, "w23")
 
         for c in range(CHUNKS):
             relu_b = keep.tile([P, CHUNK, PACK], F32, name=f"relu_b{c}")
-            nc.scalar.activation(relu_b[:], banks[c][1], ACT.Relu)
+            pieces = [slice(0, CHUNK // 2), slice(CHUNK // 2, CHUNK)] if c == 0 else [slice(0, CHUNK)]
+            for v in pieces:
+                nc.scalar.activation(relu_b[:, v, :], banks[c][1][:, v, :], ACT.Relu)
             bands = []
             for name, op in (("low", ALU.add), ("high", ALU.subtract)):
                 values = keep.tile([P, CHUNK, PACK], BF16, name=f"{name}{c}", align_bytes=64)
-                nc.vector.scalar_tensor_tensor(values[:], banks[c][0], 0.0, relu_b[:], ALU.max, op)
+                for v in pieces if name == "low" else [slice(0, CHUNK)]:
+                    nc.vector.scalar_tensor_tensor(values[:, v, :], banks[c][0][:, v, :], 0.0, relu_b[:, v, :], ALU.max, op)
                 bands.append(values)
             acc = psum.tile([P, CHUNK], F32, name=f"acc{c}")
             for i, values in enumerate(bands):
                 codes, scales = quantized(values[:].rearrange("p v t -> p (v t)"), CHUNK, f"band{c}{i}")
                 nc.tensor.matmul_mx(
                     out=acc[:],
-                    lhsT=w23_q[i][0][:].bitcast(FP8X4),
-                    lhsT_scale=w23_q[i][1][:],
+                    lhsT=w23_codes[:, i * N : (i + 1) * N].bitcast(FP8X4),
+                    lhsT_scale=w23_bytes[:, i * N : (i + 1) * N],
                     rhs=codes[:].bitcast(FP8X4),
                     rhs_scale=scales[:],
                     start=(i == 0),
                     stop=(i == 1),
                 )
             result = keep.tile([P, CHUNK], F32, name=f"result{c}")
-            nc.scalar.activation(result[:], acc[:], ACT.Copy, scale=0.5)
+            if c == 0:
+                nc.scalar.activation(result[:], acc[:], ACT.Copy, scale=0.5)
+            else:
+                nc.vector.tensor_scalar_mul(result[:], acc[:], 0.5)
             nc.sync.dma_start(out[:, c * CHUNK : (c + 1) * CHUNK], result[:])

@@ -20,6 +20,7 @@ PACK = 4
 HALVES = 2
 HALF_COLS = H // HALVES
 HALF_M = HALF_COLS // PACK
+VECTOR_M = 16
 CHUNK = 128
 CHUNKS = V // CHUNK
 LIST_ROWS = 16
@@ -29,7 +30,6 @@ def tile_picked_haar_relu_p_kernel(tc, x_words, x_scales, w1, w2, w3, offs, out)
     nc = tc.nc
     with ExitStack() as ctx:
         keep = ctx.enter_context(tc.tile_pool(name="keep", bufs=1))
-        reuse = ctx.enter_context(tc.tile_pool(name="reuse", bufs=1))
         psum = ctx.enter_context(tc.psum_pool(name="psum", bufs=1))
 
         offsets = keep.tile([P, S // LIST_ROWS], U16, name="offsets")
@@ -63,40 +63,44 @@ def tile_picked_haar_relu_p_kernel(tc, x_words, x_scales, w1, w2, w3, offs, out)
             nc.vector.quantize_mx(out=codes[:].bitcast(FP8X4), scales=scales[:], in_=values)
             return codes, scales
 
-        w1_q = {}
-        grouped = {
-            slot: reuse.tile([P, 2, P, PACK], BF16, name=f"w1_grouped{slot}", tag=f"slots{slot}", align_bytes=64) for slot in (0, 2)
-        }
+        w1_codes = keep.tile([P, PACK, P], U32, name="w1_codes", align_bytes=64)
+        w1_bytes = keep.tile([P, PACK, P], U8, name="w1_bytes", align_bytes=64)
+        w1_q = {t: (w1_codes[:, t, :], w1_bytes[:, t, :]) for t in range(PACK)}
+        grouped = [keep.tile([P, PACK, HALF_M, PACK], BF16, name=f"w1_grouped{h}", tag=f"half{h}", align_bytes=64) for h in range(HALVES)]
 
-        def deal_w1(copy, h, slot, m0, m1):
+        def deal_w1(copy, h, t0, t1, m0=0, m1=HALF_M):
             src = w1_raw[h][:].rearrange("p j (m t) -> p m t j", t=PACK)
-            dst = grouped[slot][:, :, h * HALF_M + m0 : h * HALF_M + m1, :].rearrange("p t m j -> p m t j")
-            copy(dst, src[:, m0:m1, slot : slot + 2, :])
+            copy(grouped[h][:, t0:t1, m0:m1, :].rearrange("p t m j -> p m t j"), src[:, m0:m1, t0:t1, :])
 
-        deal_w1(nc.scalar.copy, 0, 0, 0, HALF_M)
-        deal_w1(nc.scalar.copy, 0, 2, 0, HALF_M // 2)
-        deal_w1(nc.vector.tensor_copy, 0, 2, HALF_M // 2, HALF_M)
-        deal_w1(nc.vector.tensor_copy, 1, 2, 0, HALF_M)
-        deal_w1(nc.scalar.copy, 1, 0, 0, HALF_M)
-        for first_slot in (2, 0):
-            codes, scales = quantized(grouped[first_slot][:].rearrange("p t m j -> p (t m j)"), 2 * P, f"w1_{first_slot}")
-            for i in range(2):
-                w1_q[first_slot + i] = (codes[:, i * P : (i + 1) * P], scales[:, i * P : (i + 1) * P])
+        def quantize_w1(h, t):
+            cols = slice(h * HALF_M, (h + 1) * HALF_M)
+            nc.vector.quantize_mx(
+                out=w1_codes[:, t, cols].bitcast(FP8X4), scales=w1_bytes[:, t, cols], in_=grouped[h][:, t, :, :].rearrange("p m j -> p (m j)")
+            )
 
-        words_first = reuse.tile([P, CHUNK], U32, name="words_first", tag="slots2", align_bytes=64)
-        words_rest = reuse.tile([P, 3 * CHUNK], U32, name="words_rest", tag="slots0", align_bytes=64)
-        places = {"b0": words_first[:], "a0": words_rest[:, 0:CHUNK], "b1": words_rest[:, CHUNK : 2 * CHUNK], "a1": words_rest[:, 2 * CHUNK :]}
+        deal_w1(nc.scalar.copy, 0, 0, 2)
+        deal_w1(nc.scalar.copy, 0, 2, 4)
+        for t in range(PACK):
+            quantize_w1(0, t)
+        deal_w1(nc.vector.tensor_copy, 1, 0, 2)
+        deal_w1(nc.vector.tensor_copy, 1, 2, 4, 0, VECTOR_M)
+        deal_w1(nc.scalar.copy, 1, 2, 4, VECTOR_M, HALF_M)
+        for t in range(PACK):
+            quantize_w1(1, t)
+
+        words = keep.tile([P, 4 * CHUNK], U32, name="words", tag="half1", align_bytes=64)
+        places = {name: words[:, i * CHUNK : (i + 1) * CHUNK] for i, name in enumerate(("b0", "a0", "b1", "a1"))}
 
         def first_product(first, name):
-            words = places[name]
-            nc.vector.tensor_copy(words, word_table[:].indirect(offsets[:, first // LIST_ROWS : (first + CHUNK) // LIST_ROWS]))
+            picked = places[name]
+            nc.vector.tensor_copy(picked, word_table[:].indirect(offsets[:, first // LIST_ROWS : (first + CHUNK) // LIST_ROWS]))
             bank = psum.tile([P, PACK, CHUNK], F32, name=f"bank_{name}")
-            for t in (2, 3, 0, 1):
+            for t in range(PACK):
                 nc.tensor.matmul_mx(
                     out=bank[:, t, :],
                     lhsT=w1_q[t][0].bitcast(FP8X4),
                     lhsT_scale=w1_q[t][1],
-                    rhs=words.bitcast(FP8X4),
+                    rhs=picked.bitcast(FP8X4),
                     rhs_scale=x_bytes[:, first : first + CHUNK],
                     start=True,
                     stop=True,

@@ -20,7 +20,7 @@ PACK = 4
 HALVES = 2
 HALF_COLS = H // HALVES
 HALF_M = HALF_COLS // PACK
-VECTOR_M = 16
+VECTOR_M = 24
 CHUNK = 128
 CHUNKS = V // CHUNK
 LIST_ROWS = 16
@@ -35,14 +35,11 @@ def tile_picked_haar_relu_p_kernel(tc, x_words, x_scales, w1, w2, w3, offs, out)
         offsets = keep.tile([P, S // LIST_ROWS], U16, name="offsets")
         nc.sync.dma_start(offsets[:], offs)
 
-        scale_rows = keep.tile([P, T], U8, name="scale_rows")
         byte_table = keep.tile([P, T], U8, name="byte_table", align_bytes=64)
-        nc.vector.memset(byte_table[:].bitcast(I32), 0)
         for q in range(4):
-            rows = slice(32 * q, 32 * q + 4)
+            rows = slice(32 * q, 32 * q + 32)
             queue = nc.scalar if q < 2 else nc.sync
-            queue.dma_start(scale_rows[rows, :].bitcast(I32), x_scales[0, 4 * q : 4 * q + 4, :].bitcast(I32))
-            nc.vector.tensor_copy(byte_table[rows, :].bitcast(I32), scale_rows[rows, :].bitcast(I32))
+            queue.dma_start(byte_table[rows, :].bitcast(I32), x_scales[0, 4 * q : 4 * q + 4, :].bitcast(I32).partition_broadcast(8))
 
         w1_rows = w1.rearrange("(p j) c -> p j c", j=PACK)
         w1_raw = [keep.tile([P, PACK, HALF_COLS], F32, name=f"w1_raw{h}") for h in range(HALVES)]
@@ -79,7 +76,7 @@ def tile_picked_haar_relu_p_kernel(tc, x_words, x_scales, w1, w2, w3, offs, out)
             )
 
         deal_w1(nc.scalar.copy, 0, 0, 2)
-        deal_w1(nc.scalar.copy, 0, 2, 4)
+        deal_w1(nc.vector.tensor_copy, 0, 2, 4)
         for t in range(PACK):
             quantize_w1(0, t)
         deal_w1(nc.vector.tensor_copy, 1, 0, 2)

@@ -117,32 +117,44 @@ def tile_picked_haar_relu_p_kernel(tc, x_words, x_scales, w1, w2, w3, offs, out)
             )
         w23_codes, w23_bytes = quantized(w23_grouped[:].rearrange("p i n j -> p (i n j)"), 2 * N, "w23")
 
+        relu_b = [keep.tile([P, CHUNK, PACK], F32, name=f"relu_b{c}") for c in range(CHUNKS)]
+        bands = [[keep.tile([P, CHUNK, PACK], BF16, name=f"band{c}{i}", align_bytes=64) for i in range(2)] for c in range(CHUNKS)]
+        acc = [psum.tile([P, CHUNK], F32, name=f"acc{c}") for c in range(CHUNKS)]
+        ops = (ALU.add, ALU.subtract)
+        halves, whole = (slice(0, CHUNK // 2), slice(CHUNK // 2, CHUNK)), slice(0, CHUNK)
+
+        def band_from_bank(c, i, v):
+            nc.vector.scalar_tensor_tensor(bands[c][i][:, v, :], banks[c][0][:, v, :], 0.0, relu_b[c][:, v, :], ALU.max, ops[i])
+
+        def second_product(c, i):
+            codes, scales = quantized(bands[c][i][:].rearrange("p v t -> p (v t)"), CHUNK, f"band{c}{i}")
+            nc.tensor.matmul_mx(
+                out=acc[c][:],
+                lhsT=w23_codes[:, i * N : (i + 1) * N].bitcast(FP8X4),
+                lhsT_scale=w23_bytes[:, i * N : (i + 1) * N],
+                rhs=codes[:].bitcast(FP8X4),
+                rhs_scale=scales[:],
+                start=(i == 0),
+                stop=(i == 1),
+            )
+
+        for v in halves:
+            nc.scalar.activation(relu_b[0][:, v, :], banks[0][1][:, v, :], ACT.Relu)
+        nc.scalar.activation(relu_b[1][:], banks[1][1], ACT.Relu)
+        for v in halves:
+            band_from_bank(0, 0, v)
+        band_from_bank(0, 1, whole)
+        second_product(0, 0)
+        band_from_bank(1, 0, whole)
+        band_from_bank(1, 1, whole)
+        second_product(0, 1)
+        second_product(1, 0)
+        second_product(1, 1)
+
         for c in range(CHUNKS):
-            relu_b = keep.tile([P, CHUNK, PACK], F32, name=f"relu_b{c}")
-            pieces = [slice(0, CHUNK // 2), slice(CHUNK // 2, CHUNK)] if c == 0 else [slice(0, CHUNK)]
-            for v in pieces:
-                nc.scalar.activation(relu_b[:, v, :], banks[c][1][:, v, :], ACT.Relu)
-            bands = []
-            for name, op in (("low", ALU.add), ("high", ALU.subtract)):
-                values = keep.tile([P, CHUNK, PACK], BF16, name=f"{name}{c}", align_bytes=64)
-                for v in pieces if name == "low" else [slice(0, CHUNK)]:
-                    nc.vector.scalar_tensor_tensor(values[:, v, :], banks[c][0][:, v, :], 0.0, relu_b[:, v, :], ALU.max, op)
-                bands.append(values)
-            acc = psum.tile([P, CHUNK], F32, name=f"acc{c}")
-            for i, values in enumerate(bands):
-                codes, scales = quantized(values[:].rearrange("p v t -> p (v t)"), CHUNK, f"band{c}{i}")
-                nc.tensor.matmul_mx(
-                    out=acc[:],
-                    lhsT=w23_codes[:, i * N : (i + 1) * N].bitcast(FP8X4),
-                    lhsT_scale=w23_bytes[:, i * N : (i + 1) * N],
-                    rhs=codes[:].bitcast(FP8X4),
-                    rhs_scale=scales[:],
-                    start=(i == 0),
-                    stop=(i == 1),
-                )
             result = keep.tile([P, CHUNK], F32, name=f"result{c}")
             if c == 0:
-                nc.scalar.activation(result[:], acc[:], ACT.Copy, scale=0.5)
+                nc.scalar.activation(result[:], acc[c][:], ACT.Copy, scale=0.5)
             else:
-                nc.vector.tensor_scalar_mul(result[:], acc[:], 0.5)
+                nc.vector.tensor_scalar_mul(result[:], acc[c][:], 0.5)
             nc.sync.dma_start(out[:, c * CHUNK : (c + 1) * CHUNK], result[:])

@@ -17,10 +17,8 @@ ACT = mybir.ActivationFunctionType
 
 P = 128
 PACK = 4
-HALVES = 2
-HALF_COLS = H // HALVES
-HALF_M = HALF_COLS // PACK
-VECTOR_M = 24
+HALF_M = P // 2
+LAST_M = 32
 CHUNK = 128
 CHUNKS = V // CHUNK
 LIST_ROWS = 16
@@ -34,70 +32,86 @@ def tile_picked_haar_relu_p_kernel(tc, x_words, x_scales, w1, w2, w3, offs, out)
 
         offsets = keep.tile([P, S // LIST_ROWS], U16, name="offsets")
         nc.sync.dma_start(offsets[:], offs)
-
         byte_table = keep.tile([P, T], U8, name="byte_table", align_bytes=64)
         for q in range(4):
-            rows = slice(32 * q, 32 * q + 32)
             queue = nc.scalar if q < 2 else nc.sync
-            queue.dma_start(byte_table[rows, :].bitcast(I32), x_scales[0, 4 * q : 4 * q + 4, :].bitcast(I32).partition_broadcast(8))
-
-        w1_rows = w1.rearrange("(p j) c -> p j c", j=PACK)
-        w1_raw = [keep.tile([P, PACK, HALF_COLS], F32, name=f"w1_raw{h}") for h in range(HALVES)]
-        nc.sync.dma_start(w1_raw[0][:], w1_rows[:, :, 0:HALF_COLS])
-        nc.sync.dma_start(w1_raw[1][:], w1_rows[:, :, HALF_COLS:H])
+            queue.dma_start(byte_table[32 * q : 32 * q + 32, :].bitcast(I32), x_scales[0, 4 * q : 4 * q + 4, :].bitcast(I32).partition_broadcast(8))
         word_table = keep.tile([P, T], U32, name="word_table", align_bytes=64)
         nc.sync.dma_start(word_table[:].bitcast(I32), x_words[0].rearrange("p n t -> p (n t)").bitcast(I32))
+        w1_rows = w1.rearrange("(p j) c -> p j c", j=PACK)
+        split = P - LAST_M
+        w1_front = keep.tile([P, 2, H], F32, name="w1_front")
+        nc.sync.dma_start(w1_front[:], w1_rows[:, 0:2, :])
+        w1_back = keep.tile([P, 2, PACK * split], F32, name="w1_back")
+        nc.sync.dma_start(w1_back[:], w1_rows[:, 2:4, 0 : PACK * split])
+        w1_last = keep.tile([P, 2, PACK * LAST_M], F32, name="w1_last")
+        nc.sync.dma_start(w1_last[:], w1_rows[:, 2:4, PACK * split : H])
+        pieces = {"front": (w1_front, 0, 0), "back": (w1_back, 2, 0), "last": (w1_last, 2, split)}
         w23_raw = [keep.tile([P, PACK, N], F32, name=f"w23_raw{i}") for i in range(2)]
         for i, w in enumerate((w2, w3)):
             nc.sync.dma_start(w23_raw[i][:], w.rearrange("(p j) n -> p j n", j=PACK))
 
         x_bytes = keep.tile([P, S], U8, name="x_bytes", align_bytes=64)
         nc.vector.tensor_copy(x_bytes[:], byte_table[:].indirect(offsets[:]))
+        words = keep.tile([P, S], U32, name="words", align_bytes=64)
+        nc.vector.tensor_copy(words[:], word_table[:].indirect(offsets[:]))
 
-        def quantized(values, width, name):
-            codes = keep.tile([P, width], U32, name=f"{name}_codes", align_bytes=64)
-            scales = keep.tile([P, width], U8, name=f"{name}_bytes", align_bytes=64)
-            nc.vector.quantize_mx(out=codes[:].bitcast(FP8X4), scales=scales[:], in_=values)
-            return codes, scales
+        warm = psum.tile([64, S], F32, name="warm")
+        for i in range(2):
+            nc.tensor.matmul_mx(
+                out=warm[:],
+                lhsT=words[:, 0:64].bitcast(FP8X4),
+                lhsT_scale=x_bytes[:, 0:64],
+                rhs=words[:].bitcast(FP8X4),
+                rhs_scale=x_bytes[:],
+                start=True,
+                stop=True,
+            )
 
         w1_codes = keep.tile([P, PACK, P], U32, name="w1_codes", align_bytes=64)
         w1_bytes = keep.tile([P, PACK, P], U8, name="w1_bytes", align_bytes=64)
-        w1_q = {t: (w1_codes[:, t, :], w1_bytes[:, t, :]) for t in range(PACK)}
-        grouped = [keep.tile([P, PACK, HALF_M, PACK], BF16, name=f"w1_grouped{h}", tag=f"half{h}", align_bytes=64) for h in range(HALVES)]
+        grouped = {}
 
-        def deal_w1(copy, h, t0, t1, m0=0, m1=HALF_M):
-            src = w1_raw[h][:].rearrange("p j (m t) -> p m t j", t=PACK)
-            copy(grouped[h][:, t0:t1, m0:m1, :].rearrange("p t m j -> p m t j"), src[:, m0:m1, t0:t1, :])
+        def stage(h, pair, tag):
+            grouped[h, pair] = keep.tile([P, 2, HALF_M, PACK], BF16, name=f"w1_grouped{h}{pair}", tag=tag, align_bytes=64)
+
+        def deal_w1(copy, piece, pair, m0, m1):
+            raw, j0, first = pieces[piece]
+            h = m0 // HALF_M
+            src = raw[:].rearrange("p j (m t) -> p m t j", t=PACK)
+            dst = grouped[h, pair][:, :, m0 - h * HALF_M : m1 - h * HALF_M, j0 : j0 + 2].rearrange("p t m j -> p m t j")
+            copy(dst, src[:, m0 - first : m1 - first, 2 * pair : 2 * pair + 2, :])
 
         def quantize_w1(h, t):
             cols = slice(h * HALF_M, (h + 1) * HALF_M)
             nc.vector.quantize_mx(
-                out=w1_codes[:, t, cols].bitcast(FP8X4), scales=w1_bytes[:, t, cols], in_=grouped[h][:, t, :, :].rearrange("p m j -> p (m j)")
+                out=w1_codes[:, t, cols].bitcast(FP8X4),
+                scales=w1_bytes[:, t, cols],
+                in_=grouped[h, t // 2][:, t % 2, :, :].rearrange("p m j -> p (m j)"),
             )
 
-        deal_w1(nc.scalar.copy, 0, 0, 2)
-        deal_w1(nc.vector.tensor_copy, 0, 2, 4)
-        for t in range(PACK):
-            quantize_w1(0, t)
-        deal_w1(nc.vector.tensor_copy, 1, 0, 2)
-        deal_w1(nc.vector.tensor_copy, 1, 2, 4, 0, VECTOR_M)
-        deal_w1(nc.scalar.copy, 1, 2, 4, VECTOR_M, HALF_M)
-        for t in range(PACK):
-            quantize_w1(1, t)
-
-        words = keep.tile([P, 4 * CHUNK], U32, name="words", tag="half1", align_bytes=64)
-        places = {name: words[:, i * CHUNK : (i + 1) * CHUNK] for i, name in enumerate(("b0", "a0", "b1", "a1"))}
+        for h in range(2):
+            for pair in range(2):
+                stage(h, pair, f"g{h}{pair}")
+        copies = (nc.vector.tensor_copy, nc.scalar.copy)
+        for piece, m0, m1 in (("front", 0, HALF_M), ("front", HALF_M, P), ("back", 0, HALF_M), ("back", HALF_M, split)):
+            for pair in range(2):
+                deal_w1(copies[pair], piece, pair, m0, m1)
+        deal_w1(nc.vector.tensor_copy, "last", 0, split, P - 8)
+        deal_w1(nc.scalar.copy, "last", 0, P - 8, P)
+        deal_w1(nc.scalar.copy, "last", 1, split, P)
+        for h in range(2):
+            for t in range(PACK):
+                quantize_w1(h, t)
 
         def first_product(first, name):
-            picked = places[name]
-            nc.vector.tensor_copy(picked, word_table[:].indirect(offsets[:, first // LIST_ROWS : (first + CHUNK) // LIST_ROWS]))
             bank = psum.tile([P, PACK, CHUNK], F32, name=f"bank_{name}")
             for t in range(PACK):
                 nc.tensor.matmul_mx(
                     out=bank[:, t, :],
-                    lhsT=w1_q[t][0].bitcast(FP8X4),
-                    lhsT_scale=w1_q[t][1],
-                    rhs=picked.bitcast(FP8X4),
+                    lhsT=w1_codes[:, t, :].bitcast(FP8X4),
+                    lhsT_scale=w1_bytes[:, t, :],
+                    rhs=words[:, first : first + CHUNK].bitcast(FP8X4),
                     rhs_scale=x_bytes[:, first : first + CHUNK],
                     start=True,
                     stop=True,
@@ -109,13 +123,27 @@ def tile_picked_haar_relu_p_kernel(tc, x_words, x_scales, w1, w2, w3, offs, out)
             second = first_product(V + c * CHUNK, f"b{c}")
             banks.append((first_product(c * CHUNK, f"a{c}"), second))
 
-        w23_grouped = keep.tile([P, 2, N, PACK], BF16, name="w23_grouped", align_bytes=64)
-        for i in range(2):
-            nc.scalar.copy(
-                w23_grouped[:, i, :, :].rearrange("p (n i) j -> p n j i", i=4),
-                w23_raw[i][:].rearrange("p j (n i) -> p n j i", i=4),
+        def quantized(values, width, name):
+            codes = keep.tile([P, width], U32, name=f"{name}_codes", align_bytes=64)
+            scales = keep.tile([P, width], U8, name=f"{name}_bytes", align_bytes=64)
+            nc.vector.quantize_mx(out=codes[:].bitcast(FP8X4), scales=scales[:], in_=values)
+            return codes, scales
+
+        w23_grouped = [keep.tile([P, N, PACK], BF16, name=f"w23_grouped{i}", tag=("g23", "g11")[i], align_bytes=64) for i in range(2)]
+        w23_q = {}
+
+        def cast_w23(copy, i, n0, n1):
+            copy(
+                w23_grouped[i][:, n0:n1, :].rearrange("p (n i) j -> p n j i", i=4),
+                w23_raw[i][:, :, n0:n1].rearrange("p j (n i) -> p n j i", i=4),
             )
-        w23_codes, w23_bytes = quantized(w23_grouped[:].rearrange("p i n j -> p (i n j)"), 2 * N, "w23")
+
+        cast_w23(nc.scalar.copy, 0, 0, N)
+        cast_w23(nc.scalar.copy, 1, 0, N // 2)
+        cast_w23(nc.vector.tensor_copy, 1, N // 2, N)
+        for i in range(2):
+            codes, scales = quantized(w23_grouped[i][:].rearrange("p n j -> p (n j)"), N, f"w23_{i}")
+            w23_q[i] = (codes[:], scales[:])
 
         relu_b = [keep.tile([P, CHUNK, PACK], F32, name=f"relu_b{c}") for c in range(CHUNKS)]
         bands = [[keep.tile([P, CHUNK, PACK], BF16, name=f"band{c}{i}", align_bytes=64) for i in range(2)] for c in range(CHUNKS)]
@@ -130,8 +158,8 @@ def tile_picked_haar_relu_p_kernel(tc, x_words, x_scales, w1, w2, w3, offs, out)
             codes, scales = quantized(bands[c][i][:].rearrange("p v t -> p (v t)"), CHUNK, f"band{c}{i}")
             nc.tensor.matmul_mx(
                 out=acc[c][:],
-                lhsT=w23_codes[:, i * N : (i + 1) * N].bitcast(FP8X4),
-                lhsT_scale=w23_bytes[:, i * N : (i + 1) * N],
+                lhsT=w23_q[i][0].bitcast(FP8X4),
+                lhsT_scale=w23_q[i][1],
                 rhs=codes[:].bitcast(FP8X4),
                 rhs_scale=scales[:],
                 start=(i == 0),

@@ -18,8 +18,10 @@ ACT = mybir.ActivationFunctionType
 P = 128
 PACK = 4
 HALF_M = P // 2
-LAST_M = 32
+LAST_M = 64
 CHUNK = 128
+FIRST = 32
+SHARE = 72
 CHUNKS = V // CHUNK
 LIST_ROWS = 16
 
@@ -94,7 +96,7 @@ def tile_picked_haar_relu_p_kernel(tc, x_words, x_scales, w1, w2, w3, offs, out)
             for pair in range(2):
                 stage(h, pair, f"g{h}{pair}")
         copies = (nc.vector.tensor_copy, nc.scalar.copy)
-        for piece, m0, m1 in (("front", 0, HALF_M), ("front", HALF_M, P), ("back", 0, HALF_M), ("back", HALF_M, split)):
+        for piece, m0, m1 in (("front", 0, HALF_M), ("front", HALF_M, P), ("back", 0, HALF_M)):
             for pair in range(2):
                 deal_w1(copies[pair], piece, pair, m0, m1)
         deal_w1(nc.vector.tensor_copy, "last", 0, split, P - 8)
@@ -123,8 +125,8 @@ def tile_picked_haar_relu_p_kernel(tc, x_words, x_scales, w1, w2, w3, offs, out)
             second = first_product(V + c * CHUNK, f"b{c}")
             banks.append((first_product(c * CHUNK, f"a{c}"), second))
 
-        def quantized(values, width, name):
-            codes = keep.tile([P, width], U32, name=f"{name}_codes", align_bytes=64)
+        def quantized(values, width, name, tag=None):
+            codes = keep.tile([P, width], U32, name=f"{name}_codes", tag=tag or f"{name}_codes", align_bytes=64)
             scales = keep.tile([P, width], U8, name=f"{name}_bytes", align_bytes=64)
             nc.vector.quantize_mx(out=codes[:].bitcast(FP8X4), scales=scales[:], in_=values)
             return codes, scales
@@ -145,17 +147,19 @@ def tile_picked_haar_relu_p_kernel(tc, x_words, x_scales, w1, w2, w3, offs, out)
             codes, scales = quantized(w23_grouped[i][:].rearrange("p n j -> p (n j)"), N, f"w23_{i}")
             w23_q[i] = (codes[:], scales[:])
 
-        relu_b = [keep.tile([P, CHUNK, PACK], F32, name=f"relu_b{c}") for c in range(CHUNKS)]
+        relu_b = [keep.tile([P, CHUNK, PACK], F32, name=f"relu_b{c}", tag=f"relu_b{c}", align_bytes=64) for c in range(CHUNKS)]
+        relu_a = keep.tile([P, CHUNK - SHARE, PACK], F32, name="relu_a", tag="relu_a", align_bytes=64)
         bands = [[keep.tile([P, CHUNK, PACK], BF16, name=f"band{c}{i}", align_bytes=64) for i in range(2)] for c in range(CHUNKS)]
         acc = [psum.tile([P, CHUNK], F32, name=f"acc{c}") for c in range(CHUNKS)]
         ops = (ALU.add, ALU.subtract)
-        halves, whole = (slice(0, CHUNK // 2), slice(CHUNK // 2, CHUNK)), slice(0, CHUNK)
+        opening, whole = (slice(0, FIRST), slice(FIRST, CHUNK)), slice(0, CHUNK)
+        mine, shared = slice(0, SHARE), slice(SHARE, CHUNK)
 
         def band_from_bank(c, i, v):
             nc.vector.scalar_tensor_tensor(bands[c][i][:, v, :], banks[c][0][:, v, :], 0.0, relu_b[c][:, v, :], ALU.max, ops[i])
 
-        def second_product(c, i):
-            codes, scales = quantized(bands[c][i][:].rearrange("p v t -> p (v t)"), CHUNK, f"band{c}{i}")
+        def second_product(c, i, tag=None):
+            codes, scales = quantized(bands[c][i][:].rearrange("p v t -> p (v t)"), CHUNK, f"band{c}{i}", tag)
             nc.tensor.matmul_mx(
                 out=acc[c][:],
                 lhsT=w23_q[i][0].bitcast(FP8X4),
@@ -166,16 +170,20 @@ def tile_picked_haar_relu_p_kernel(tc, x_words, x_scales, w1, w2, w3, offs, out)
                 stop=(i == 1),
             )
 
-        for v in halves:
+        for v in opening:
             nc.scalar.activation(relu_b[0][:, v, :], banks[0][1][:, v, :], ACT.Relu)
-        nc.scalar.activation(relu_b[1][:], banks[1][1], ACT.Relu)
-        for v in halves:
-            band_from_bank(0, 0, v)
-        band_from_bank(0, 1, whole)
-        second_product(0, 0)
+        nc.scalar.activation(relu_b[1][:, shared, :], banks[1][1][:, shared, :], ACT.Relu)
+        nc.scalar.activation(relu_a[:], banks[1][0][:, shared, :], ACT.Relu)
+        nc.gpsimd.tensor_tensor(bands[1][1][:, shared, :], relu_a[:], relu_b[1][:, shared, :], ops[1])
+        nc.scalar.activation(relu_b[1][:, mine, :], banks[1][1][:, mine, :], ACT.Relu)
+        band_from_bank(0, 0, opening[0])
+        band_from_bank(0, 1, opening[0])
+        band_from_bank(0, 0, opening[1])
+        band_from_bank(0, 1, opening[1])
         band_from_bank(1, 0, whole)
-        band_from_bank(1, 1, whole)
-        second_product(0, 1)
+        band_from_bank(1, 1, mine)
+        second_product(0, 0, "relu_a")
+        second_product(0, 1, "relu_b1")
         second_product(1, 0)
         second_product(1, 1)
 

@@ -18,11 +18,12 @@ ACT = mybir.ActivationFunctionType
 P = 128
 PACK = 4
 HALF_M = P // 2
-LAST_M = 64
 CHUNK = 128
-FIRST = 32
-SHARE = 72
 CHUNKS = V // CHUNK
+OPENING = (0, 32, CHUNK)
+SHARED = 56
+TAIL_M = -16
+WARM_M = 64
 LIST_ROWS = 16
 
 
@@ -41,14 +42,11 @@ def tile_picked_haar_relu_p_kernel(tc, x_words, x_scales, w1, w2, w3, offs, out)
         word_table = keep.tile([P, T], U32, name="word_table", align_bytes=64)
         nc.sync.dma_start(word_table[:].bitcast(I32), x_words[0].rearrange("p n t -> p (n t)").bitcast(I32))
         w1_rows = w1.rearrange("(p j) c -> p j c", j=PACK)
-        split = P - LAST_M
         w1_front = keep.tile([P, 2, H], F32, name="w1_front")
         nc.sync.dma_start(w1_front[:], w1_rows[:, 0:2, :])
-        w1_back = keep.tile([P, 2, PACK * split], F32, name="w1_back")
-        nc.sync.dma_start(w1_back[:], w1_rows[:, 2:4, 0 : PACK * split])
-        w1_last = keep.tile([P, 2, PACK * LAST_M], F32, name="w1_last")
-        nc.sync.dma_start(w1_last[:], w1_rows[:, 2:4, PACK * split : H])
-        pieces = {"front": (w1_front, 0, 0), "back": (w1_back, 2, 0), "last": (w1_last, 2, split)}
+        w1_back = [keep.tile([P, 2, H // 2], F32, name=f"w1_back{h}") for h in range(2)]
+        for h in range(2):
+            nc.sync.dma_start(w1_back[h][:], w1_rows[:, 2:4, h * H // 2 : (h + 1) * H // 2])
         w23_raw = [keep.tile([P, PACK, N], F32, name=f"w23_raw{i}") for i in range(2)]
         for i, w in enumerate((w2, w3)):
             nc.sync.dma_start(w23_raw[i][:], w.rearrange("(p j) n -> p j n", j=PACK))
@@ -58,12 +56,12 @@ def tile_picked_haar_relu_p_kernel(tc, x_words, x_scales, w1, w2, w3, offs, out)
         words = keep.tile([P, S], U32, name="words", align_bytes=64)
         nc.vector.tensor_copy(words[:], word_table[:].indirect(offsets[:]))
 
-        warm = psum.tile([64, S], F32, name="warm")
+        warm = psum.tile([WARM_M, S], F32, name="warm")
         for i in range(2):
             nc.tensor.matmul_mx(
                 out=warm[:],
-                lhsT=words[:, 0:64].bitcast(FP8X4),
-                lhsT_scale=x_bytes[:, 0:64],
+                lhsT=words[:, 0:WARM_M].bitcast(FP8X4),
+                lhsT_scale=x_bytes[:, 0:WARM_M],
                 rhs=words[:].bitcast(FP8X4),
                 rhs_scale=x_bytes[:],
                 start=True,
@@ -72,43 +70,37 @@ def tile_picked_haar_relu_p_kernel(tc, x_words, x_scales, w1, w2, w3, offs, out)
 
         w1_codes = keep.tile([P, PACK, P], U32, name="w1_codes", align_bytes=64)
         w1_bytes = keep.tile([P, PACK, P], U8, name="w1_bytes", align_bytes=64)
-        grouped = {}
+        grouped = {
+            (h, pair): keep.tile([P, 2, HALF_M, PACK], BF16, name=f"w1_grouped{h}{pair}", tag=f"g{h}{pair}", align_bytes=64)
+            for h in range(2)
+            for pair in range(2)
+        }
 
-        def stage(h, pair, tag):
-            grouped[h, pair] = keep.tile([P, 2, HALF_M, PACK], BF16, name=f"w1_grouped{h}{pair}", tag=tag, align_bytes=64)
-
-        def deal_w1(copy, piece, pair, m0, m1):
-            raw, j0, first = pieces[piece]
+        def deal_w1(copy, raw, first, j0, pair, m0, m1):
             h = m0 // HALF_M
             src = raw[:].rearrange("p j (m t) -> p m t j", t=PACK)
             dst = grouped[h, pair][:, :, m0 - h * HALF_M : m1 - h * HALF_M, j0 : j0 + 2].rearrange("p t m j -> p m t j")
             copy(dst, src[:, m0 - first : m1 - first, 2 * pair : 2 * pair + 2, :])
 
-        def quantize_w1(h, t):
-            cols = slice(h * HALF_M, (h + 1) * HALF_M)
-            nc.vector.quantize_mx(
-                out=w1_codes[:, t, cols].bitcast(FP8X4),
-                scales=w1_bytes[:, t, cols],
-                in_=grouped[h, t // 2][:, t % 2, :, :].rearrange("p m j -> p (m j)"),
-            )
-
-        for h in range(2):
-            for pair in range(2):
-                stage(h, pair, f"g{h}{pair}")
         copies = (nc.vector.tensor_copy, nc.scalar.copy)
-        for piece, m0, m1 in (("front", 0, HALF_M), ("front", HALF_M, P), ("back", 0, HALF_M)):
+        for raw, j0, m0 in ((w1_front, 0, 0), (w1_front, 0, HALF_M), (w1_back[0], 2, 0)):
             for pair in range(2):
-                deal_w1(copies[pair], piece, pair, m0, m1)
-        deal_w1(nc.vector.tensor_copy, "last", 0, split, P - 8)
-        deal_w1(nc.scalar.copy, "last", 0, P - 8, P)
-        deal_w1(nc.scalar.copy, "last", 1, split, P)
+                deal_w1(copies[pair], raw, 0, j0, pair, m0, m0 + HALF_M)
+        deal_w1(nc.vector.tensor_copy, w1_back[1], HALF_M, 2, 0, HALF_M, P)
+        deal_w1(nc.vector.tensor_copy, w1_back[1], HALF_M, 2, 1, HALF_M, HALF_M - TAIL_M)
+        deal_w1(nc.scalar.copy, w1_back[1], HALF_M, 2, 1, HALF_M - TAIL_M, P)
         for h in range(2):
+            cols = slice(h * HALF_M, (h + 1) * HALF_M)
             for t in range(PACK):
-                quantize_w1(h, t)
+                nc.vector.quantize_mx(
+                    out=w1_codes[:, t, cols].bitcast(FP8X4),
+                    scales=w1_bytes[:, t, cols],
+                    in_=grouped[h, t // 2][:, t % 2, :, :].rearrange("p m j -> p (m j)"),
+                )
 
-        def first_product(first, name):
-            bank = psum.tile([P, PACK, CHUNK], F32, name=f"bank_{name}")
-            for t in range(PACK):
+        def first_product(first, name, slots):
+            bank = psum.tile([P, PACK, CHUNK], F32, name=name)
+            for t in slots:
                 nc.tensor.matmul_mx(
                     out=bank[:, t, :],
                     lhsT=w1_codes[:, t, :].bitcast(FP8X4),
@@ -120,77 +112,75 @@ def tile_picked_haar_relu_p_kernel(tc, x_words, x_scales, w1, w2, w3, offs, out)
                 )
             return bank[:].rearrange("p t v -> p v t")
 
-        banks = []
-        for c in range(CHUNKS):
-            second = first_product(V + c * CHUNK, f"b{c}")
-            banks.append((first_product(c * CHUNK, f"a{c}"), second))
+        rising = list(range(PACK))
+        falling = rising[::-1]
+        bank_b0 = first_product(V, "bank_b0", rising)
+        bank_a0 = first_product(0, "bank_a0", falling)
+        bank_a1 = first_product(CHUNK, "bank_a1", falling)
+        bank_b1 = first_product(V + CHUNK, "bank_b1", falling)
+        banks_a = (bank_a0, bank_a1)
 
-        def quantized(values, width, name, tag=None):
-            codes = keep.tile([P, width], U32, name=f"{name}_codes", tag=tag or f"{name}_codes", align_bytes=64)
+        def quantized(values, width, name, tag):
+            codes = keep.tile([P, width], U32, name=f"{name}_codes", tag=tag, align_bytes=64)
             scales = keep.tile([P, width], U8, name=f"{name}_bytes", align_bytes=64)
             nc.vector.quantize_mx(out=codes[:].bitcast(FP8X4), scales=scales[:], in_=values)
             return codes, scales
 
         w23_grouped = [keep.tile([P, N, PACK], BF16, name=f"w23_grouped{i}", tag=("g23", "g11")[i], align_bytes=64) for i in range(2)]
-        w23_q = {}
-
-        def cast_w23(copy, i, n0, n1):
+        for i, copy in enumerate((nc.scalar.copy, nc.vector.tensor_copy)):
             copy(
-                w23_grouped[i][:, n0:n1, :].rearrange("p (n i) j -> p n j i", i=4),
-                w23_raw[i][:, :, n0:n1].rearrange("p j (n i) -> p n j i", i=4),
+                w23_grouped[i][:].rearrange("p (n i) j -> p n j i", i=4),
+                w23_raw[i][:].rearrange("p j (n i) -> p n j i", i=4),
             )
-
-        cast_w23(nc.scalar.copy, 0, 0, N)
-        cast_w23(nc.scalar.copy, 1, 0, N // 2)
-        cast_w23(nc.vector.tensor_copy, 1, N // 2, N)
-        for i in range(2):
-            codes, scales = quantized(w23_grouped[i][:].rearrange("p n j -> p (n j)"), N, f"w23_{i}")
-            w23_q[i] = (codes[:], scales[:])
+        w2_q = quantized(w23_grouped[0][:].rearrange("p n j -> p (n j)"), N, "w2", "w2_codes")
+        w3_q = quantized(w23_grouped[1][:].rearrange("p n j -> p (n j)"), N, "w3", "w3_codes")
 
         relu_b = [keep.tile([P, CHUNK, PACK], F32, name=f"relu_b{c}", tag=f"relu_b{c}", align_bytes=64) for c in range(CHUNKS)]
-        relu_a = keep.tile([P, CHUNK - SHARE, PACK], F32, name="relu_a", tag="relu_a", align_bytes=64)
-        bands = [[keep.tile([P, CHUNK, PACK], BF16, name=f"band{c}{i}", align_bytes=64) for i in range(2)] for c in range(CHUNKS)]
-        acc = [psum.tile([P, CHUNK], F32, name=f"acc{c}") for c in range(CHUNKS)]
+        relu_a = keep.tile([P, SHARED, PACK], F32, name="relu_a", tag="relu_a", align_bytes=64)
+        bands = [keep.tile([P, 2, CHUNK, PACK], BF16, name=f"bands{c}", align_bytes=64) for c in range(CHUNKS)]
         ops = (ALU.add, ALU.subtract)
-        opening, whole = (slice(0, FIRST), slice(FIRST, CHUNK)), slice(0, CHUNK)
-        mine, shared = slice(0, SHARE), slice(SHARE, CHUNK)
+        opening = [slice(v0, v1) for v0, v1 in zip(OPENING, OPENING[1:])]
+        shared, mine = slice(0, SHARED), slice(SHARED, CHUNK)
 
         def band_from_bank(c, i, v):
-            nc.vector.scalar_tensor_tensor(bands[c][i][:, v, :], banks[c][0][:, v, :], 0.0, relu_b[c][:, v, :], ALU.max, ops[i])
-
-        def second_product(c, i, tag=None):
-            codes, scales = quantized(bands[c][i][:].rearrange("p v t -> p (v t)"), CHUNK, f"band{c}{i}", tag)
-            nc.tensor.matmul_mx(
-                out=acc[c][:],
-                lhsT=w23_q[i][0].bitcast(FP8X4),
-                lhsT_scale=w23_q[i][1],
-                rhs=codes[:].bitcast(FP8X4),
-                rhs_scale=scales[:],
-                start=(i == 0),
-                stop=(i == 1),
-            )
+            nc.vector.scalar_tensor_tensor(bands[c][:, i, v, :], banks_a[c][:, v, :], 0.0, relu_b[c][:, v, :], ALU.max, ops[i])
 
         for v in opening:
-            nc.scalar.activation(relu_b[0][:, v, :], banks[0][1][:, v, :], ACT.Relu)
-        nc.scalar.activation(relu_b[1][:, shared, :], banks[1][1][:, shared, :], ACT.Relu)
-        nc.scalar.activation(relu_a[:], banks[1][0][:, shared, :], ACT.Relu)
-        nc.gpsimd.tensor_tensor(bands[1][1][:, shared, :], relu_a[:], relu_b[1][:, shared, :], ops[1])
-        nc.scalar.activation(relu_b[1][:, mine, :], banks[1][1][:, mine, :], ACT.Relu)
-        band_from_bank(0, 0, opening[0])
-        band_from_bank(0, 1, opening[0])
-        band_from_bank(0, 0, opening[1])
-        band_from_bank(0, 1, opening[1])
-        band_from_bank(1, 0, whole)
-        band_from_bank(1, 1, mine)
-        second_product(0, 0, "relu_a")
-        second_product(0, 1, "relu_b1")
-        second_product(1, 0)
-        second_product(1, 1)
+            nc.scalar.activation(relu_b[0][:, v, :], bank_b0[:, v, :], ACT.Relu)
+        nc.scalar.activation(relu_a[:], bank_a1[:, shared, :], ACT.Relu)
+        for v in (shared, mine):
+            nc.scalar.activation(relu_b[1][:, v, :], bank_b1[:, v, :], ACT.Relu)
+        nc.gpsimd.tensor_tensor(bands[1][:, 1, shared, :], relu_a[:], relu_b[1][:, shared, :], ops[1])
+        for v in opening:
+            for i in range(2):
+                band_from_bank(0, i, v)
+        band_from_bank(1, 0, shared)
+        for i in range(2):
+            band_from_bank(1, i, mine)
 
+        first_q = quantized(bands[0][:].rearrange("p i v t -> p (i v t)"), 2 * CHUNK, "bands0", "relu_a")
+        moving = [
+            [(first_q[0][:, i * CHUNK : (i + 1) * CHUNK], first_q[1][:, i * CHUNK : (i + 1) * CHUNK]) for i in range(2)],
+            [
+                [part[:] for part in quantized(bands[1][:, i, :, :].rearrange("p v t -> p (v t)"), CHUNK, f"bands1{i}", f"bands1{i}_codes")]
+                for i in range(2)
+            ],
+        ]
         for c in range(CHUNKS):
+            acc = psum.tile([P, CHUNK], F32, name=f"acc{c}")
+            for i, (codes, scales) in enumerate((w2_q, w3_q)):
+                nc.tensor.matmul_mx(
+                    out=acc[:],
+                    lhsT=codes[:].bitcast(FP8X4),
+                    lhsT_scale=scales[:],
+                    rhs=moving[c][i][0].bitcast(FP8X4),
+                    rhs_scale=moving[c][i][1],
+                    start=(i == 0),
+                    stop=(i == 1),
+                )
             result = keep.tile([P, CHUNK], F32, name=f"result{c}")
             if c == 0:
-                nc.scalar.activation(result[:], acc[c][:], ACT.Copy, scale=0.5)
+                nc.scalar.activation(result[:], acc[:], ACT.Copy, scale=0.5)
             else:
-                nc.vector.tensor_scalar_mul(result[:], acc[c][:], 0.5)
+                nc.vector.tensor_scalar_mul(result[:], acc[:], 0.5)
             nc.sync.dma_start(out[:, c * CHUNK : (c + 1) * CHUNK], result[:])

@@ -21,9 +21,6 @@ HALF_M = P // 2
 CHUNK = 128
 CHUNKS = V // CHUNK
 OPENING = (0, 32, CHUNK)
-SHARED = 56
-TAIL_M = -16
-WARM_M = 64
 LIST_ROWS = 16
 
 
@@ -36,88 +33,77 @@ def tile_picked_haar_relu_p_kernel(tc, x_words, x_scales, w1, w2, w3, offs, out)
         offsets = keep.tile([P, S // LIST_ROWS], U16, name="offsets")
         nc.sync.dma_start(offsets[:], offs)
         byte_table = keep.tile([P, T], U8, name="byte_table", align_bytes=64)
+        nc.vector.memset(byte_table[:].bitcast(I32), 0)
+        staged = keep.tile([P, T], U8, name="staged", align_bytes=64)
         for q in range(4):
             queue = nc.scalar if q < 2 else nc.sync
-            queue.dma_start(byte_table[32 * q : 32 * q + 32, :].bitcast(I32), x_scales[0, 4 * q : 4 * q + 4, :].bitcast(I32).partition_broadcast(8))
-        word_table = keep.tile([P, T], U32, name="word_table", align_bytes=64)
-        nc.sync.dma_start(word_table[:].bitcast(I32), x_words[0].rearrange("p n t -> p (n t)").bitcast(I32))
+            queue.dma_start(staged[32 * q : 32 * q + 4, :].bitcast(I32), x_scales[0, 4 * q : 4 * q + 4, :].bitcast(I32))
         w1_rows = w1.rearrange("(p j) c -> p j c", j=PACK)
-        w1_front = keep.tile([P, 2, H], F32, name="w1_front")
+        w1_front = keep.tile([P, 2, H], F32, name="w1_front", tag="front", align_bytes=64)
         nc.sync.dma_start(w1_front[:], w1_rows[:, 0:2, :])
         w1_back = [keep.tile([P, 2, H // 2], F32, name=f"w1_back{h}") for h in range(2)]
         for h in range(2):
             nc.sync.dma_start(w1_back[h][:], w1_rows[:, 2:4, h * H // 2 : (h + 1) * H // 2])
+        word_table = keep.tile([P, T], U32, name="word_table", align_bytes=64)
+        nc.sync.dma_start(word_table[:].bitcast(I32), x_words[0].rearrange("p n t -> p (n t)").bitcast(I32))
         w23_raw = [keep.tile([P, PACK, N], F32, name=f"w23_raw{i}") for i in range(2)]
         for i, w in enumerate((w2, w3)):
             nc.sync.dma_start(w23_raw[i][:], w.rearrange("(p j) n -> p j n", j=PACK))
 
+        for q in range(4):
+            rows = slice(32 * q, 32 * q + 4)
+            nc.vector.tensor_copy(byte_table[rows, :].bitcast(I32), staged[rows, :].bitcast(I32))
         x_bytes = keep.tile([P, S], U8, name="x_bytes", align_bytes=64)
         nc.vector.tensor_copy(x_bytes[:], byte_table[:].indirect(offsets[:]))
-        words = keep.tile([P, S], U32, name="words", align_bytes=64)
-        nc.vector.tensor_copy(words[:], word_table[:].indirect(offsets[:]))
-
-        warm = psum.tile([WARM_M, S], F32, name="warm")
-        for i in range(2):
-            nc.tensor.matmul_mx(
-                out=warm[:],
-                lhsT=words[:, 0:WARM_M].bitcast(FP8X4),
-                lhsT_scale=x_bytes[:, 0:WARM_M],
-                rhs=words[:].bitcast(FP8X4),
-                rhs_scale=x_bytes[:],
-                start=True,
-                stop=True,
-            )
 
         w1_codes = keep.tile([P, PACK, P], U32, name="w1_codes", align_bytes=64)
         w1_bytes = keep.tile([P, PACK, P], U8, name="w1_bytes", align_bytes=64)
-        grouped = {
-            (h, pair): keep.tile([P, 2, HALF_M, PACK], BF16, name=f"w1_grouped{h}{pair}", tag=f"g{h}{pair}", align_bytes=64)
-            for h in range(2)
-            for pair in range(2)
-        }
+        grouped = keep.tile([P, PACK, P, PACK], BF16, name="w1_grouped", tag="g1", align_bytes=64)
 
-        def deal_w1(copy, raw, first, j0, pair, m0, m1):
-            h = m0 // HALF_M
-            src = raw[:].rearrange("p j (m t) -> p m t j", t=PACK)
-            dst = grouped[h, pair][:, :, m0 - h * HALF_M : m1 - h * HALF_M, j0 : j0 + 2].rearrange("p t m j -> p m t j")
-            copy(dst, src[:, m0 - first : m1 - first, 2 * pair : 2 * pair + 2, :])
+        def deal_w1(copy, raw, j0, pair, cols):
+            src = raw.rearrange("p j (m t) -> p m t j", t=PACK)
+            dst = grouped[:, 2 * pair : 2 * pair + 2, cols, j0 : j0 + 2].rearrange("p t m j -> p m t j")
+            copy(dst, src[:, :, 2 * pair : 2 * pair + 2, :])
 
-        copies = (nc.vector.tensor_copy, nc.scalar.copy)
-        for raw, j0, m0 in ((w1_front, 0, 0), (w1_front, 0, HALF_M), (w1_back[0], 2, 0)):
-            for pair in range(2):
-                deal_w1(copies[pair], raw, 0, j0, pair, m0, m0 + HALF_M)
-        deal_w1(nc.vector.tensor_copy, w1_back[1], HALF_M, 2, 0, HALF_M, P)
-        deal_w1(nc.vector.tensor_copy, w1_back[1], HALF_M, 2, 1, HALF_M, HALF_M - TAIL_M)
-        deal_w1(nc.scalar.copy, w1_back[1], HALF_M, 2, 1, HALF_M - TAIL_M, P)
+        def gpsimd_cast(dst, src):
+            nc.gpsimd.tensor_scalar(dst, src, 1.0, 0.0, ALU.mult, ALU.add)
+
+        for pair, copy in enumerate((nc.scalar.copy, gpsimd_cast)):
+            deal_w1(copy, w1_front[:], 0, pair, slice(0, P))
         for h in range(2):
             cols = slice(h * HALF_M, (h + 1) * HALF_M)
+            for pair, copy in enumerate((nc.vector.tensor_copy, nc.scalar.copy)):
+                deal_w1(copy, w1_back[h][:], 2, pair, cols)
             for t in range(PACK):
                 nc.vector.quantize_mx(
                     out=w1_codes[:, t, cols].bitcast(FP8X4),
                     scales=w1_bytes[:, t, cols],
-                    in_=grouped[h, t // 2][:, t % 2, :, :].rearrange("p m j -> p (m j)"),
+                    in_=grouped[:, t, cols, :].rearrange("p m j -> p (m j)"),
                 )
 
-        def first_product(first, name, slots):
+        words = keep.tile([P, S], U32, name="words", tag="g1", align_bytes=64)
+
+        def first_product(first, name, picked):
+            entries = slice(first, first + CHUNK)
+            listed = offsets[:, first // LIST_ROWS : (first + CHUNK) // LIST_ROWS]
+            nc.vector.tensor_copy(picked, word_table[:].indirect(listed))
             bank = psum.tile([P, PACK, CHUNK], F32, name=name)
-            for t in slots:
+            for t in range(PACK):
                 nc.tensor.matmul_mx(
                     out=bank[:, t, :],
                     lhsT=w1_codes[:, t, :].bitcast(FP8X4),
                     lhsT_scale=w1_bytes[:, t, :],
-                    rhs=words[:, first : first + CHUNK].bitcast(FP8X4),
-                    rhs_scale=x_bytes[:, first : first + CHUNK],
+                    rhs=picked.bitcast(FP8X4),
+                    rhs_scale=x_bytes[:, entries],
                     start=True,
                     stop=True,
                 )
             return bank[:].rearrange("p t v -> p v t")
 
-        rising = list(range(PACK))
-        falling = rising[::-1]
-        bank_b0 = first_product(V, "bank_b0", rising)
-        bank_a0 = first_product(0, "bank_a0", falling)
-        bank_a1 = first_product(CHUNK, "bank_a1", falling)
-        bank_b1 = first_product(V + CHUNK, "bank_b1", falling)
+        bank_b0 = first_product(V, "bank_b0", words[:, 0:CHUNK])
+        bank_a0 = first_product(0, "bank_a0", words[:, 1 * CHUNK : 2 * CHUNK])
+        bank_b1 = first_product(V + CHUNK, "bank_b1", words[:, 2 * CHUNK : 3 * CHUNK])
+        bank_a1 = first_product(CHUNK, "bank_a1", words[:, 3 * CHUNK : 4 * CHUNK])
         banks_a = (bank_a0, bank_a1)
 
         def quantized(values, width, name, tag):
@@ -126,46 +112,39 @@ def tile_picked_haar_relu_p_kernel(tc, x_words, x_scales, w1, w2, w3, offs, out)
             nc.vector.quantize_mx(out=codes[:].bitcast(FP8X4), scales=scales[:], in_=values)
             return codes, scales
 
-        w23_grouped = [keep.tile([P, N, PACK], BF16, name=f"w23_grouped{i}", tag=("g23", "g11")[i], align_bytes=64) for i in range(2)]
-        for i, copy in enumerate((nc.scalar.copy, nc.vector.tensor_copy)):
+        w23_both = keep.tile([P, 2, N, PACK], BF16, name="w23_grouped", tag="front", align_bytes=64)
+        w23_grouped = [w23_both[:, i, :, :] for i in range(2)]
+        for i, copy in enumerate((nc.scalar.copy, nc.scalar.copy)):
             copy(
-                w23_grouped[i][:].rearrange("p (n i) j -> p n j i", i=4),
+                w23_grouped[i].rearrange("p (n i) j -> p n j i", i=4),
                 w23_raw[i][:].rearrange("p j (n i) -> p n j i", i=4),
             )
-        w2_q = quantized(w23_grouped[0][:].rearrange("p n j -> p (n j)"), N, "w2", "w2_codes")
-        w3_q = quantized(w23_grouped[1][:].rearrange("p n j -> p (n j)"), N, "w3", "w3_codes")
+        w2_q = quantized(w23_grouped[0].rearrange("p n j -> p (n j)"), N, "w2", "w2_codes")
+        w3_q = quantized(w23_grouped[1].rearrange("p n j -> p (n j)"), N, "w3", "w3_codes")
 
         relu_b = [keep.tile([P, CHUNK, PACK], F32, name=f"relu_b{c}", tag=f"relu_b{c}", align_bytes=64) for c in range(CHUNKS)]
-        relu_a = keep.tile([P, SHARED, PACK], F32, name="relu_a", tag="relu_a", align_bytes=64)
         bands = [keep.tile([P, 2, CHUNK, PACK], BF16, name=f"bands{c}", align_bytes=64) for c in range(CHUNKS)]
         ops = (ALU.add, ALU.subtract)
         opening = [slice(v0, v1) for v0, v1 in zip(OPENING, OPENING[1:])]
-        shared, mine = slice(0, SHARED), slice(SHARED, CHUNK)
 
         def band_from_bank(c, i, v):
             nc.vector.scalar_tensor_tensor(bands[c][:, i, v, :], banks_a[c][:, v, :], 0.0, relu_b[c][:, v, :], ALU.max, ops[i])
 
         for v in opening:
             nc.scalar.activation(relu_b[0][:, v, :], bank_b0[:, v, :], ACT.Relu)
-        nc.scalar.activation(relu_a[:], bank_a1[:, shared, :], ACT.Relu)
-        for v in (shared, mine):
-            nc.scalar.activation(relu_b[1][:, v, :], bank_b1[:, v, :], ACT.Relu)
-        nc.gpsimd.tensor_tensor(bands[1][:, 1, shared, :], relu_a[:], relu_b[1][:, shared, :], ops[1])
+        nc.scalar.activation(relu_b[1][:], bank_b1, ACT.Relu)
+
+        def quantized_band(c, i):
+            return [part[:] for part in quantized(bands[c][:, i, :, :].rearrange("p v t -> p (v t)"), CHUNK, f"bands{c}{i}", f"bands{c}{i}_codes")]
+
         for v in opening:
             for i in range(2):
                 band_from_bank(0, i, v)
-        band_from_bank(1, 0, shared)
+        moving = [[quantized_band(0, 0)], []]
         for i in range(2):
-            band_from_bank(1, i, mine)
-
-        first_q = quantized(bands[0][:].rearrange("p i v t -> p (i v t)"), 2 * CHUNK, "bands0", "relu_a")
-        moving = [
-            [(first_q[0][:, i * CHUNK : (i + 1) * CHUNK], first_q[1][:, i * CHUNK : (i + 1) * CHUNK]) for i in range(2)],
-            [
-                [part[:] for part in quantized(bands[1][:, i, :, :].rearrange("p v t -> p (v t)"), CHUNK, f"bands1{i}", f"bands1{i}_codes")]
-                for i in range(2)
-            ],
-        ]
+            band_from_bank(1, i, slice(0, CHUNK))
+        moving[0].append(quantized_band(0, 1))
+        moving[1].extend(quantized_band(1, i) for i in range(2))
         for c in range(CHUNKS):
             acc = psum.tile([P, CHUNK], F32, name=f"acc{c}")
             for i, (codes, scales) in enumerate((w2_q, w3_q)):

@@ -41,9 +41,12 @@ def tile_picked_haar_relu_p_kernel(tc, x_words, x_scales, w1, w2, w3, offs, out)
         w1_rows = w1.rearrange("(p j) c -> p j c", j=PACK)
         w1_front = keep.tile([P, 2, H], F32, name="w1_front", tag="front", align_bytes=64)
         nc.sync.dma_start(w1_front[:], w1_rows[:, 0:2, :])
-        w1_back = [keep.tile([P, 2, H // 2], F32, name=f"w1_back{h}") for h in range(2)]
-        for h in range(2):
-            nc.sync.dma_start(w1_back[h][:], w1_rows[:, 2:4, h * H // 2 : (h + 1) * H // 2])
+        w1_back = keep.tile([P, 2, H], F32, name="w1_back")
+        back_run = w1_back[:].rearrange("p j c -> p (j c)")
+        w1_run = w1.rearrange("(p j) c -> p (j c)", j=PACK)
+        cut = H + H // 2
+        nc.sync.dma_start(back_run[:, 0:cut], w1_run[:, 2 * H : 2 * H + cut])
+        nc.sync.dma_start(back_run[:, cut:], w1_run[:, 2 * H + cut :])
         word_table = keep.tile([P, T], U32, name="word_table", align_bytes=64)
         nc.sync.dma_start(word_table[:].bitcast(I32), x_words[0].rearrange("p n t -> p (n t)").bitcast(I32))
         w23_raw = [keep.tile([P, PACK, N], F32, name=f"w23_raw{i}") for i in range(2)]
@@ -73,7 +76,9 @@ def tile_picked_haar_relu_p_kernel(tc, x_words, x_scales, w1, w2, w3, offs, out)
         for h in range(2):
             cols = slice(h * HALF_M, (h + 1) * HALF_M)
             for pair, copy in enumerate((nc.vector.tensor_copy, nc.scalar.copy)):
-                deal_w1(copy, w1_back[h][:], 2, pair, cols)
+                deal_w1(copy, w1_back[:, :, h * H // 2 : (h + 1) * H // 2], 2, pair, cols)
+        for h in range(2):
+            cols = slice(h * HALF_M, (h + 1) * HALF_M)
             for t in range(PACK):
                 nc.vector.quantize_mx(
                     out=w1_codes[:, t, cols].bitcast(FP8X4),

@@ -19,15 +19,16 @@ P = 128
 PACK = 4
 HALF_M = P // 2
 CHUNK = 128
-CHUNKS = V // CHUNK
-OPENING = (0, 32, CHUNK)
+OPENING = 32
 LIST_ROWS = 16
+WORDS_BYTES = 4 * CHUNK
 
 
 def tile_picked_haar_relu_p_kernel(tc, x_words, x_scales, w1, w2, w3, offs, out):
     nc = tc.nc
     with ExitStack() as ctx:
         keep = ctx.enter_context(tc.tile_pool(name="keep", bufs=1))
+        shared = ctx.enter_context(tc.tile_pool(name="shared", bufs=1))
         psum = ctx.enter_context(tc.psum_pool(name="psum", bufs=1))
 
         offsets = keep.tile([P, S // LIST_ROWS], U16, name="offsets")
@@ -38,12 +39,11 @@ def tile_picked_haar_relu_p_kernel(tc, x_words, x_scales, w1, w2, w3, offs, out)
         for q in range(4):
             queue = nc.scalar if q < 2 else nc.sync
             queue.dma_start(staged[32 * q : 32 * q + 4, :].bitcast(I32), x_scales[0, 4 * q : 4 * q + 4, :].bitcast(I32))
-        w1_rows = w1.rearrange("(p j) c -> p j c", j=PACK)
-        w1_front = keep.tile([P, 2, H], F32, name="w1_front", tag="front", align_bytes=64)
-        nc.sync.dma_start(w1_front[:], w1_rows[:, 0:2, :])
-        w1_back = keep.tile([P, 2, H], F32, name="w1_back")
-        back_run = w1_back[:].rearrange("p j c -> p (j c)")
         w1_run = w1.rearrange("(p j) c -> p (j c)", j=PACK)
+        w1_front = keep.tile([P, 2, H], F32, name="w1_front", tag="front", align_bytes=64)
+        nc.sync.dma_start(w1_front[:].rearrange("p j c -> p (j c)"), w1_run[:, 0 : 2 * H])
+        w1_back = keep.tile([P, 2, H], F32, name="w1_back", align_bytes=64)
+        back_run = w1_back[:].rearrange("p j c -> p (j c)")
         cut = H + H // 2
         nc.sync.dma_start(back_run[:, 0:cut], w1_run[:, 2 * H : 2 * H + cut])
         nc.sync.dma_start(back_run[:, cut:], w1_run[:, 2 * H + cut :])
@@ -53,18 +53,21 @@ def tile_picked_haar_relu_p_kernel(tc, x_words, x_scales, w1, w2, w3, offs, out)
         for i, w in enumerate((w2, w3)):
             nc.sync.dma_start(w23_raw[i][:], w.rearrange("(p j) n -> p j n", j=PACK))
 
+        def listed(first, count):
+            return offsets[:, first // LIST_ROWS : (first + count) // LIST_ROWS]
+
         for q in range(4):
             rows = slice(32 * q, 32 * q + 4)
             nc.vector.tensor_copy(byte_table[rows, :].bitcast(I32), staged[rows, :].bitcast(I32))
-        x_bytes = keep.tile([P, S], U8, name="x_bytes", align_bytes=64)
-        nc.vector.tensor_copy(x_bytes[:], byte_table[:].indirect(offsets[:]))
+        early_bytes = keep.tile([P, S - CHUNK], U8, name="early_bytes", align_bytes=64)
+        nc.vector.tensor_copy(early_bytes[:], byte_table[:].indirect(listed(CHUNK, S - CHUNK)))
 
         w1_codes = keep.tile([P, PACK, P], U32, name="w1_codes", align_bytes=64)
         w1_bytes = keep.tile([P, PACK, P], U8, name="w1_bytes", align_bytes=64)
-        grouped = keep.tile([P, PACK, P, PACK], BF16, name="w1_grouped", tag="g1", align_bytes=64)
+        grouped = shared.tile([P, PACK, P, PACK], BF16, name="w1_grouped", align_bytes=64, offset=0)
 
         def deal_w1(copy, raw, j0, pair, cols):
-            src = raw.rearrange("p j (m t) -> p m t j", t=PACK)
+            src = raw[:, :, PACK * cols.start : PACK * cols.stop].rearrange("p j (m t) -> p m t j", t=PACK)
             dst = grouped[:, 2 * pair : 2 * pair + 2, cols, j0 : j0 + 2].rearrange("p t m j -> p m t j")
             copy(dst, src[:, :, 2 * pair : 2 * pair + 2, :])
 
@@ -72,11 +75,10 @@ def tile_picked_haar_relu_p_kernel(tc, x_words, x_scales, w1, w2, w3, offs, out)
             nc.gpsimd.tensor_scalar(dst, src, 1.0, 0.0, ALU.mult, ALU.add)
 
         for pair, copy in enumerate((nc.scalar.copy, gpsimd_cast)):
-            deal_w1(copy, w1_front[:], 0, pair, slice(0, P))
+            deal_w1(copy, w1_front, 0, pair, slice(0, P))
         for h in range(2):
-            cols = slice(h * HALF_M, (h + 1) * HALF_M)
             for pair, copy in enumerate((nc.vector.tensor_copy, nc.scalar.copy)):
-                deal_w1(copy, w1_back[:, :, h * H // 2 : (h + 1) * H // 2], 2, pair, cols)
+                deal_w1(copy, w1_back, 2, pair, slice(h * HALF_M, (h + 1) * HALF_M))
         for h in range(2):
             cols = slice(h * HALF_M, (h + 1) * HALF_M)
             for t in range(PACK):
@@ -86,61 +88,61 @@ def tile_picked_haar_relu_p_kernel(tc, x_words, x_scales, w1, w2, w3, offs, out)
                     in_=grouped[:, t, cols, :].rearrange("p m j -> p (m j)"),
                 )
 
-        words = keep.tile([P, S], U32, name="words", tag="g1", align_bytes=64)
+        firsts = (V + CHUNK, CHUNK, V, 0)
+        words = []
+        for n, first in enumerate(firsts):
+            picked = shared.tile([P, CHUNK], U32, name=f"words{n}", align_bytes=64, offset=n * WORDS_BYTES)
+            nc.vector.tensor_copy(picked[:], word_table[:].indirect(listed(first, CHUNK)))
+            words.append(picked)
 
-        def first_product(first, name, picked):
-            entries = slice(first, first + CHUNK)
-            listed = offsets[:, first // LIST_ROWS : (first + CHUNK) // LIST_ROWS]
-            nc.vector.tensor_copy(picked, word_table[:].indirect(listed))
-            bank = psum.tile([P, PACK, CHUNK], F32, name=name)
+        def first_product(n, scales):
+            bank = psum.tile([P, PACK, CHUNK], F32, name=f"bank{n}")
             for t in range(PACK):
                 nc.tensor.matmul_mx(
                     out=bank[:, t, :],
                     lhsT=w1_codes[:, t, :].bitcast(FP8X4),
                     lhsT_scale=w1_bytes[:, t, :],
-                    rhs=picked.bitcast(FP8X4),
-                    rhs_scale=x_bytes[:, entries],
+                    rhs=words[n][:].bitcast(FP8X4),
+                    rhs_scale=scales,
                     start=True,
                     stop=True,
                 )
             return bank[:].rearrange("p t v -> p v t")
 
-        bank_b0 = first_product(V, "bank_b0", words[:, 0:CHUNK])
-        bank_a0 = first_product(0, "bank_a0", words[:, 1 * CHUNK : 2 * CHUNK])
-        bank_b1 = first_product(V + CHUNK, "bank_b1", words[:, 2 * CHUNK : 3 * CHUNK])
-        bank_a1 = first_product(CHUNK, "bank_a1", words[:, 3 * CHUNK : 4 * CHUNK])
-        banks_a = (bank_a0, bank_a1)
+        banks = [first_product(n, early_bytes[:, first - CHUNK : first]) for n, first in enumerate(firsts[:3])]
 
-        def quantized(values, width, name, tag):
-            codes = keep.tile([P, width], U32, name=f"{name}_codes", tag=tag, align_bytes=64)
+        def quantized(values, width, name):
+            codes = keep.tile([P, width], U32, name=f"{name}_codes", align_bytes=64)
             scales = keep.tile([P, width], U8, name=f"{name}_bytes", align_bytes=64)
             nc.vector.quantize_mx(out=codes[:].bitcast(FP8X4), scales=scales[:], in_=values)
             return codes, scales
 
-        w23_both = keep.tile([P, 2, N, PACK], BF16, name="w23_grouped", tag="front", align_bytes=64)
-        w23_grouped = [w23_both[:, i, :, :] for i in range(2)]
-        for i, copy in enumerate((nc.scalar.copy, nc.scalar.copy)):
-            copy(
-                w23_grouped[i].rearrange("p (n i) j -> p n j i", i=4),
+        w23_grouped = keep.tile([P, 2, N, PACK], BF16, name="w23_grouped", tag="front", align_bytes=64)
+        for i in range(2):
+            nc.scalar.copy(
+                w23_grouped[:, i, :, :].rearrange("p (n i) j -> p n j i", i=4),
                 w23_raw[i][:].rearrange("p j (n i) -> p n j i", i=4),
             )
-        w2_q = quantized(w23_grouped[0].rearrange("p n j -> p (n j)"), N, "w2", "w2_codes")
-        w3_q = quantized(w23_grouped[1].rearrange("p n j -> p (n j)"), N, "w3", "w3_codes")
+        w2_q = quantized(w23_grouped[:, 0, :, :].rearrange("p n j -> p (n j)"), N, "w2")
+        late_bytes = shared.tile([P, CHUNK], U8, name="late_bytes", align_bytes=64, offset=0)
+        nc.vector.tensor_copy(late_bytes[:], byte_table[:].indirect(listed(0, CHUNK)))
+        banks.append(first_product(3, late_bytes[:]))
+        w3_q = quantized(w23_grouped[:, 1, :, :].rearrange("p n j -> p (n j)"), N, "w3")
 
-        relu_b = [keep.tile([P, CHUNK, PACK], F32, name=f"relu_b{c}", tag=f"relu_b{c}", align_bytes=64) for c in range(CHUNKS)]
-        bands = [keep.tile([P, 2, CHUNK, PACK], BF16, name=f"bands{c}", align_bytes=64) for c in range(CHUNKS)]
+        relu_b = [keep.tile([P, CHUNK, PACK], F32, name=f"relu_b{c}", align_bytes=64) for c in range(2)]
+        bands = [keep.tile([P, 2, CHUNK, PACK], BF16, name=f"bands{c}", align_bytes=64) for c in range(2)]
         ops = (ALU.add, ALU.subtract)
-        opening = [slice(v0, v1) for v0, v1 in zip(OPENING, OPENING[1:])]
+        opening = (slice(0, OPENING), slice(OPENING, CHUNK))
 
         def band_from_bank(c, i, v):
-            nc.vector.scalar_tensor_tensor(bands[c][:, i, v, :], banks_a[c][:, v, :], 0.0, relu_b[c][:, v, :], ALU.max, ops[i])
+            nc.vector.scalar_tensor_tensor(bands[c][:, i, v, :], banks[2 * c + 1][:, v, :], 0.0, relu_b[c][:, v, :], ALU.max, ops[i])
 
         for v in opening:
-            nc.scalar.activation(relu_b[0][:, v, :], bank_b0[:, v, :], ACT.Relu)
-        nc.scalar.activation(relu_b[1][:], bank_b1, ACT.Relu)
+            nc.scalar.activation(relu_b[0][:, v, :], banks[0][:, v, :], ACT.Relu)
+        nc.scalar.activation(relu_b[1][:], banks[2], ACT.Relu)
 
         def quantized_band(c, i):
-            return [part[:] for part in quantized(bands[c][:, i, :, :].rearrange("p v t -> p (v t)"), CHUNK, f"bands{c}{i}", f"bands{c}{i}_codes")]
+            return quantized(bands[c][:, i, :, :].rearrange("p v t -> p (v t)"), CHUNK, f"bands{c}{i}")
 
         for v in opening:
             for i in range(2):
@@ -150,15 +152,15 @@ def tile_picked_haar_relu_p_kernel(tc, x_words, x_scales, w1, w2, w3, offs, out)
             band_from_bank(1, i, slice(0, CHUNK))
         moving[0].append(quantized_band(0, 1))
         moving[1].extend(quantized_band(1, i) for i in range(2))
-        for c in range(CHUNKS):
+        for c in range(2):
             acc = psum.tile([P, CHUNK], F32, name=f"acc{c}")
             for i, (codes, scales) in enumerate((w2_q, w3_q)):
                 nc.tensor.matmul_mx(
                     out=acc[:],
                     lhsT=codes[:].bitcast(FP8X4),
                     lhsT_scale=scales[:],
-                    rhs=moving[c][i][0].bitcast(FP8X4),
-                    rhs_scale=moving[c][i][1],
+                    rhs=moving[c][i][0][:].bitcast(FP8X4),
+                    rhs_scale=moving[c][i][1][:],
                     start=(i == 0),
                     stop=(i == 1),
                 )
@@ -167,4 +169,5 @@ def tile_picked_haar_relu_p_kernel(tc, x_words, x_scales, w1, w2, w3, offs, out)
                 nc.scalar.activation(result[:], acc[:], ACT.Copy, scale=0.5)
             else:
                 nc.vector.tensor_scalar_mul(result[:], acc[:], 0.5)
-            nc.sync.dma_start(out[:, c * CHUNK : (c + 1) * CHUNK], result[:])
+            first = firsts[2 * c + 1]
+            nc.sync.dma_start(out[:, first : first + CHUNK], result[:])

@@ -34,13 +34,16 @@ def tile_picked_haar_relu_p_kernel(tc, x_words, x_scales, w1, w2, w3, offs, out)
         offsets = keep.tile([P, S // LIST_ROWS], U16, name="offsets")
         nc.sync.dma_start(offsets[:], offs)
         byte_table = keep.tile([P, T], U8, name="byte_table", align_bytes=64)
-        nc.vector.memset(byte_table[:].bitcast(I32), 0)
+        nc.vector.memset(byte_table[64:, :].bitcast(I32), 0)
         staged = keep.tile([P, T], U8, name="staged", align_bytes=64)
-        for q in range(4):
-            queue = nc.scalar if q < 2 else nc.sync
-            queue.dma_start(staged[32 * q : 32 * q + 4, :].bitcast(I32), x_scales[0, 4 * q : 4 * q + 4, :].bitcast(I32))
+        for q, queue in enumerate((nc.scalar, nc.sync, nc.scalar, nc.sync)):
+            rows = x_scales[0, 4 * q : 4 * q + 4, :].bitcast(I32)
+            if q < 2:
+                queue.dma_start(byte_table[32 * q : 32 * q + 32, :].bitcast(I32), rows.partition_broadcast(8))
+            else:
+                queue.dma_start(staged[32 * q : 32 * q + 4, :].bitcast(I32), rows)
         w1_run = w1.rearrange("(p j) c -> p (j c)", j=PACK)
-        w1_front = keep.tile([P, 2, H], F32, name="w1_front", tag="front", align_bytes=64)
+        w1_front = shared.tile([P, 2, H], F32, name="w1_front", align_bytes=64, offset=0)
         nc.sync.dma_start(w1_front[:].rearrange("p j c -> p (j c)"), w1_run[:, 0 : 2 * H])
         w1_back = keep.tile([P, 2, H], F32, name="w1_back", align_bytes=64)
         back_run = w1_back[:].rearrange("p j c -> p (j c)")
@@ -56,15 +59,15 @@ def tile_picked_haar_relu_p_kernel(tc, x_words, x_scales, w1, w2, w3, offs, out)
         def listed(first, count):
             return offsets[:, first // LIST_ROWS : (first + count) // LIST_ROWS]
 
-        for q in range(4):
+        for q in range(2, 4):
             rows = slice(32 * q, 32 * q + 4)
             nc.vector.tensor_copy(byte_table[rows, :].bitcast(I32), staged[rows, :].bitcast(I32))
-        early_bytes = keep.tile([P, S - CHUNK], U8, name="early_bytes", align_bytes=64)
-        nc.vector.tensor_copy(early_bytes[:], byte_table[:].indirect(listed(CHUNK, S - CHUNK)))
+        x_bytes = keep.tile([P, S], U8, name="x_bytes", align_bytes=64)
+        nc.vector.tensor_copy(x_bytes[:], byte_table[:].indirect(offsets[:]))
 
         w1_codes = keep.tile([P, PACK, P], U32, name="w1_codes", align_bytes=64)
         w1_bytes = keep.tile([P, PACK, P], U8, name="w1_bytes", align_bytes=64)
-        grouped = shared.tile([P, PACK, P, PACK], BF16, name="w1_grouped", align_bytes=64, offset=0)
+        grouped = keep.tile([P, PACK, P, PACK], BF16, name="w1_grouped", align_bytes=64)
 
         def deal_w1(copy, raw, j0, pair, cols):
             src = raw[:, :, PACK * cols.start : PACK * cols.stop].rearrange("p j (m t) -> p m t j", t=PACK)
@@ -79,9 +82,10 @@ def tile_picked_haar_relu_p_kernel(tc, x_words, x_scales, w1, w2, w3, offs, out)
         for h in range(2):
             for pair, copy in enumerate((nc.vector.tensor_copy, nc.scalar.copy)):
                 deal_w1(copy, w1_back, 2, pair, slice(h * HALF_M, (h + 1) * HALF_M))
-        for h in range(2):
+
+        def quantize_w1(h, slots):
             cols = slice(h * HALF_M, (h + 1) * HALF_M)
-            for t in range(PACK):
+            for t in slots:
                 nc.vector.quantize_mx(
                     out=w1_codes[:, t, cols].bitcast(FP8X4),
                     scales=w1_bytes[:, t, cols],
@@ -89,11 +93,15 @@ def tile_picked_haar_relu_p_kernel(tc, x_words, x_scales, w1, w2, w3, offs, out)
                 )
 
         firsts = (V + CHUNK, CHUNK, V, 0)
-        words = []
-        for n, first in enumerate(firsts):
+
+        def gathered_words(n):
             picked = shared.tile([P, CHUNK], U32, name=f"words{n}", align_bytes=64, offset=n * WORDS_BYTES)
-            nc.vector.tensor_copy(picked[:], word_table[:].indirect(listed(first, CHUNK)))
-            words.append(picked)
+            nc.vector.tensor_copy(picked[:], word_table[:].indirect(listed(firsts[n], CHUNK)))
+            return picked
+
+        for h in range(2):
+            quantize_w1(h, range(PACK))
+        words = [gathered_words(n) for n in range(4)]
 
         def first_product(n, scales):
             bank = psum.tile([P, PACK, CHUNK], F32, name=f"bank{n}")
@@ -109,7 +117,7 @@ def tile_picked_haar_relu_p_kernel(tc, x_words, x_scales, w1, w2, w3, offs, out)
                 )
             return bank[:].rearrange("p t v -> p v t")
 
-        banks = [first_product(n, early_bytes[:, first - CHUNK : first]) for n, first in enumerate(firsts[:3])]
+        banks = [first_product(n, x_bytes[:, first : first + CHUNK]) for n, first in enumerate(firsts)]
 
         def quantized(values, width, name):
             codes = keep.tile([P, width], U32, name=f"{name}_codes", align_bytes=64)
@@ -117,16 +125,13 @@ def tile_picked_haar_relu_p_kernel(tc, x_words, x_scales, w1, w2, w3, offs, out)
             nc.vector.quantize_mx(out=codes[:].bitcast(FP8X4), scales=scales[:], in_=values)
             return codes, scales
 
-        w23_grouped = keep.tile([P, 2, N, PACK], BF16, name="w23_grouped", tag="front", align_bytes=64)
+        w23_grouped = shared.tile([P, 2, N, PACK], BF16, name="w23_grouped", align_bytes=64, offset=4 * WORDS_BYTES)
         for i in range(2):
             nc.scalar.copy(
                 w23_grouped[:, i, :, :].rearrange("p (n i) j -> p n j i", i=4),
                 w23_raw[i][:].rearrange("p j (n i) -> p n j i", i=4),
             )
         w2_q = quantized(w23_grouped[:, 0, :, :].rearrange("p n j -> p (n j)"), N, "w2")
-        late_bytes = shared.tile([P, CHUNK], U8, name="late_bytes", align_bytes=64, offset=0)
-        nc.vector.tensor_copy(late_bytes[:], byte_table[:].indirect(listed(0, CHUNK)))
-        banks.append(first_product(3, late_bytes[:]))
         w3_q = quantized(w23_grouped[:, 1, :, :].rearrange("p n j -> p (n j)"), N, "w3")
 
         relu_b = [keep.tile([P, CHUNK, PACK], F32, name=f"relu_b{c}", align_bytes=64) for c in range(2)]

@@ -31,17 +31,14 @@ def tile_picked_haar_relu_p_kernel(tc, x_words, x_scales, w1, w2, w3, offs, out)
         shared = ctx.enter_context(tc.tile_pool(name="shared", bufs=1))
         psum = ctx.enter_context(tc.psum_pool(name="psum", bufs=1))
 
+        byte_table = keep.tile([P, T], U8, name="byte_table", align_bytes=64)
+        nc.vector.memset(byte_table[:].bitcast(I32), 0)
+        staged = keep.tile([P, T], U8, name="staged", align_bytes=64)
+        for q in range(4):
+            queue = nc.sync if q < 2 else nc.scalar
+            queue.dma_start(staged[32 * q : 32 * q + 4, :].bitcast(I32), x_scales[0, 4 * q : 4 * q + 4, :].bitcast(I32))
         offsets = keep.tile([P, S // LIST_ROWS], U16, name="offsets")
         nc.sync.dma_start(offsets[:], offs)
-        byte_table = keep.tile([P, T], U8, name="byte_table", align_bytes=64)
-        nc.vector.memset(byte_table[64:, :].bitcast(I32), 0)
-        staged = keep.tile([P, T], U8, name="staged", align_bytes=64)
-        for q, queue in enumerate((nc.scalar, nc.sync, nc.scalar, nc.sync)):
-            rows = x_scales[0, 4 * q : 4 * q + 4, :].bitcast(I32)
-            if q < 2:
-                queue.dma_start(byte_table[32 * q : 32 * q + 32, :].bitcast(I32), rows.partition_broadcast(8))
-            else:
-                queue.dma_start(staged[32 * q : 32 * q + 4, :].bitcast(I32), rows)
         w1_run = w1.rearrange("(p j) c -> p (j c)", j=PACK)
         w1_front = shared.tile([P, 2, H], F32, name="w1_front", align_bytes=64, offset=0)
         nc.sync.dma_start(w1_front[:].rearrange("p j c -> p (j c)"), w1_run[:, 0 : 2 * H])
@@ -59,7 +56,7 @@ def tile_picked_haar_relu_p_kernel(tc, x_words, x_scales, w1, w2, w3, offs, out)
         def listed(first, count):
             return offsets[:, first // LIST_ROWS : (first + count) // LIST_ROWS]
 
-        for q in range(2, 4):
+        for q in range(4):
             rows = slice(32 * q, 32 * q + 4)
             nc.vector.tensor_copy(byte_table[rows, :].bitcast(I32), staged[rows, :].bitcast(I32))
         x_bytes = keep.tile([P, S], U8, name="x_bytes", align_bytes=64)

@@ -123,11 +123,12 @@ def tile_picked_haar_relu_p_kernel(tc, x_words, x_scales, w1, w2, w3, offs, out)
             return codes, scales
 
         w23_grouped = shared.tile([P, 2, N, PACK], BF16, name="w23_grouped", align_bytes=64, offset=4 * WORDS_BYTES)
-        for i in range(2):
+        for i, cols in ((0, slice(0, N)), (1, slice(0, N // 2))):
             nc.scalar.copy(
-                w23_grouped[:, i, :, :].rearrange("p (n i) j -> p n j i", i=4),
-                w23_raw[i][:].rearrange("p j (n i) -> p n j i", i=4),
+                w23_grouped[:, i, cols, :].rearrange("p (n i) j -> p n j i", i=4),
+                w23_raw[i][:, :, cols].rearrange("p j (n i) -> p n j i", i=4),
             )
+        gpsimd_cast(w23_grouped[:, 1, N // 2 :, :], w23_raw[1][:, :, N // 2 :].rearrange("p j n -> p n j"))
         w2_q = quantized(w23_grouped[:, 0, :, :].rearrange("p n j -> p (n j)"), N, "w2")
         w3_q = quantized(w23_grouped[:, 1, :, :].rearrange("p n j -> p (n j)"), N, "w3")
 

@@ -21,6 +21,7 @@ HALF_M = P // 2
 CHUNK = 128
 OPENING = 32
 LIST_ROWS = 16
+HALF = CHUNK // 2
 WORDS_BYTES = 4 * CHUNK
 
 
@@ -89,32 +90,43 @@ def tile_picked_haar_relu_p_kernel(tc, x_words, x_scales, w1, w2, w3, offs, out)
                     in_=grouped[:, t, cols, :].rearrange("p m j -> p (m j)"),
                 )
 
-        firsts = (V + CHUNK, CHUNK, V, 0)
-
-        def gathered_words(n):
-            picked = shared.tile([P, CHUNK], U32, name=f"words{n}", align_bytes=64, offset=n * WORDS_BYTES)
-            nc.vector.tensor_copy(picked[:], word_table[:].indirect(listed(firsts[n], CHUNK)))
-            return picked
-
+        mixed_bytes = keep.tile([P, 2, 2, HALF], U8, name="mixed_bytes", align_bytes=64)
+        nc.vector.tensor_copy(
+            mixed_bytes[:].bitcast(I32),
+            x_bytes[:].bitcast(I32).rearrange("p (d c h w) -> p c h d w", d=2, c=2, h=2)[:, 0],
+        )
         for h in range(2):
             quantize_w1(h, range(PACK))
-        words = [gathered_words(n) for n in range(4)]
 
-        def first_product(n, scales):
-            bank = psum.tile([P, PACK, CHUNK], F32, name=f"bank{n}")
+        plain_words = []
+        for n, first in enumerate((V + CHUNK, CHUNK)):
+            picked = shared.tile([P, CHUNK], U32, name=f"words{n}", align_bytes=64, offset=n * WORDS_BYTES)
+            nc.vector.tensor_copy(picked[:], word_table[:].indirect(listed(first, CHUNK)))
+            plain_words.append(picked)
+        mixed_words = shared.tile([P, 2, 2, HALF], U32, name="mixed_words", align_bytes=64, offset=2 * WORDS_BYTES)
+        for d in range(2):
+            nc.vector.tensor_copy(mixed_words[:, :, d, :], word_table[:].indirect(listed(d * V, CHUNK)))
+
+        def first_product(name, words, scales):
+            bank = psum.tile([P, PACK, CHUNK], F32, name=name)
             for t in range(PACK):
                 nc.tensor.matmul_mx(
                     out=bank[:, t, :],
                     lhsT=w1_codes[:, t, :].bitcast(FP8X4),
                     lhsT_scale=w1_bytes[:, t, :],
-                    rhs=words[n][:].bitcast(FP8X4),
+                    rhs=words.bitcast(FP8X4),
                     rhs_scale=scales,
                     start=True,
                     stop=True,
                 )
             return bank[:].rearrange("p t v -> p v t")
 
-        banks = [first_product(n, x_bytes[:, first : first + CHUNK]) for n, first in enumerate(firsts)]
+        upper_b = first_product("upper_b", plain_words[0][:], x_bytes[:, V + CHUNK :])
+        upper_a = first_product("upper_a", plain_words[1][:], x_bytes[:, CHUNK:V])
+        mixed = [
+            first_product(f"mixed{h}", mixed_words[:, h].rearrange("p d v -> p (d v)"), mixed_bytes[:, h].rearrange("p d v -> p (d v)"))
+            for h in range(2)
+        ]
 
         def quantized(values, width, name):
             codes = keep.tile([P, width], U32, name=f"{name}_codes", align_bytes=64)
@@ -132,45 +144,51 @@ def tile_picked_haar_relu_p_kernel(tc, x_words, x_scales, w1, w2, w3, offs, out)
         w2_q = quantized(w23_grouped[:, 0, :, :].rearrange("p n j -> p (n j)"), N, "w2")
         w3_q = quantized(w23_grouped[:, 1, :, :].rearrange("p n j -> p (n j)"), N, "w3")
 
-        relu_b = [keep.tile([P, CHUNK, PACK], F32, name=f"relu_b{c}", align_bytes=64) for c in range(2)]
-        bands = [keep.tile([P, 2, CHUNK, PACK], BF16, name=f"bands{c}", align_bytes=64) for c in range(2)]
-        ops = (ALU.add, ALU.subtract)
+        upper_relu_b = keep.tile([P, CHUNK, PACK], F32, name="upper_relu_b", align_bytes=64)
+        relu_both = keep.tile([P, CHUNK, PACK], F32, name="relu_both", align_bytes=64)
+        last_relu_b = keep.tile([P, HALF, PACK], F32, name="last_relu_b", align_bytes=64)
         opening = (slice(0, OPENING), slice(OPENING, CHUNK))
-
-        def band_from_bank(c, i, v):
-            nc.vector.scalar_tensor_tensor(bands[c][:, i, v, :], banks[2 * c + 1][:, v, :], 0.0, relu_b[c][:, v, :], ALU.max, ops[i])
-
         for v in opening:
-            nc.scalar.activation(relu_b[0][:, v, :], banks[0][:, v, :], ACT.Relu)
-        nc.scalar.activation(relu_b[1][:], banks[2], ACT.Relu)
+            nc.scalar.activation(upper_relu_b[:, v, :], upper_b[:, v, :], ACT.Relu)
+        nc.scalar.activation(relu_both[:], mixed[0], ACT.Relu)
+        nc.scalar.activation(last_relu_b[:], mixed[1][:, HALF:, :], ACT.Relu)
 
-        def quantized_band(c, i):
-            return quantized(bands[c][:, i, :, :].rearrange("p v t -> p (v t)"), CHUNK, f"bands{c}{i}")
+        def band(dst, a_in_bank, relu_b, op):
+            nc.vector.scalar_tensor_tensor(dst, a_in_bank, 0.0, relu_b, ALU.max, op)
 
+        def quantized_band(values, name):
+            return quantized(values[:].rearrange("p v t -> p (v t)"), CHUNK, name)
+
+        upper_low = keep.tile([P, CHUNK, PACK], BF16, name="upper_low", tag="band", align_bytes=64)
+        upper_high = keep.tile([P, CHUNK, PACK], BF16, name="upper_high", align_bytes=64)
         for v in opening:
-            for i in range(2):
-                band_from_bank(0, i, v)
-        moving = [[quantized_band(0, 0)], []]
-        for i in range(2):
-            band_from_bank(1, i, slice(0, CHUNK))
-        moving[0].append(quantized_band(0, 1))
-        moving[1].extend(quantized_band(1, i) for i in range(2))
-        for c in range(2):
-            acc = psum.tile([P, CHUNK], F32, name=f"acc{c}")
+            band(upper_low[:, v, :], upper_a[:, v, :], upper_relu_b[:, v, :], ALU.add)
+            band(upper_high[:, v, :], upper_a[:, v, :], upper_relu_b[:, v, :], ALU.subtract)
+        upper_q = (quantized_band(upper_low, "upper_low"), quantized_band(upper_high, "upper_high"))
+
+        lower_low = keep.tile([P, CHUNK, PACK], BF16, name="lower_low", align_bytes=64)
+        lower_high = keep.tile([P, CHUNK, PACK], BF16, name="lower_high", tag="band", align_bytes=64)
+        nc.gpsimd.tensor_tensor(lower_high[:, :HALF, :], relu_both[:, :HALF, :], relu_both[:, HALF:, :], ALU.subtract)
+        band(lower_low[:, :HALF, :], mixed[0][:, :HALF, :], relu_both[:, HALF:, :], ALU.add)
+        band(lower_low[:, HALF:, :], mixed[1][:, :HALF, :], last_relu_b[:], ALU.add)
+        band(lower_high[:, HALF:, :], mixed[1][:, :HALF, :], last_relu_b[:], ALU.subtract)
+        lower_q = (quantized_band(lower_low, "lower_low"), quantized_band(lower_high, "lower_high"))
+
+        for first, moving in ((CHUNK, upper_q), (0, lower_q)):
+            acc = psum.tile([P, CHUNK], F32, name=f"acc{first}")
             for i, (codes, scales) in enumerate((w2_q, w3_q)):
                 nc.tensor.matmul_mx(
                     out=acc[:],
                     lhsT=codes[:].bitcast(FP8X4),
                     lhsT_scale=scales[:],
-                    rhs=moving[c][i][0][:].bitcast(FP8X4),
-                    rhs_scale=moving[c][i][1][:],
+                    rhs=moving[i][0][:].bitcast(FP8X4),
+                    rhs_scale=moving[i][1][:],
                     start=(i == 0),
                     stop=(i == 1),
                 )
-            result = keep.tile([P, CHUNK], F32, name=f"result{c}")
-            if c == 0:
+            result = keep.tile([P, CHUNK], F32, name=f"result{first}")
+            if first:
                 nc.scalar.activation(result[:], acc[:], ACT.Copy, scale=0.5)
             else:
                 nc.vector.tensor_scalar_mul(result[:], acc[:], 0.5)
-            first = firsts[2 * c + 1]
             nc.sync.dma_start(out[:, first : first + CHUNK], result[:])

@@ -19,7 +19,6 @@ P = 128
 PACK = 4
 HALF_M = P // 2
 CHUNK = 128
-OPENING = 32
 LIST_ROWS = 16
 HALF = CHUNK // 2
 WORDS_BYTES = 4 * CHUNK
@@ -33,7 +32,7 @@ def tile_picked_haar_relu_p_kernel(tc, x_words, x_scales, w1, w2, w3, offs, out)
         psum = ctx.enter_context(tc.psum_pool(name="psum", bufs=1))
 
         byte_table = keep.tile([P, T], U8, name="byte_table", align_bytes=64)
-        nc.vector.memset(byte_table[:].bitcast(I32), 0)
+        nc.gpsimd.memset(byte_table[:].bitcast(I32), 0)
         staged = keep.tile([P, T], U8, name="staged", align_bytes=64)
         for q in range(4):
             queue = nc.sync if q < 2 else nc.scalar
@@ -128,8 +127,8 @@ def tile_picked_haar_relu_p_kernel(tc, x_words, x_scales, w1, w2, w3, offs, out)
             for h in range(2)
         ]
 
-        def quantized(values, width, name):
-            codes = keep.tile([P, width], U32, name=f"{name}_codes", align_bytes=64)
+        def quantized(values, width, name, tag=""):
+            codes = keep.tile([P, width], U32, name=f"{name}_codes", tag=tag, align_bytes=64)
             scales = keep.tile([P, width], U8, name=f"{name}_bytes", align_bytes=64)
             nc.vector.quantize_mx(out=codes[:].bitcast(FP8X4), scales=scales[:], in_=values)
             return codes, scales
@@ -141,14 +140,13 @@ def tile_picked_haar_relu_p_kernel(tc, x_words, x_scales, w1, w2, w3, offs, out)
                 w23_raw[i][:, :, cols].rearrange("p j (n i) -> p n j i", i=4),
             )
         gpsimd_cast(w23_grouped[:, 1, N // 2 :, :], w23_raw[1][:, :, N // 2 :].rearrange("p j n -> p n j"))
-        w2_q = quantized(w23_grouped[:, 0, :, :].rearrange("p n j -> p (n j)"), N, "w2")
-        w3_q = quantized(w23_grouped[:, 1, :, :].rearrange("p n j -> p (n j)"), N, "w3")
+        w23_codes, w23_bytes = quantized(w23_grouped[:].rearrange("p i n j -> p (i n j)"), 2 * N, "w23")
 
         upper_relu_b = keep.tile([P, CHUNK, PACK], F32, name="upper_relu_b", align_bytes=64)
-        relu_both = keep.tile([P, CHUNK, PACK], F32, name="relu_both", align_bytes=64)
+        relu_both = keep.tile([P, CHUNK, PACK], F32, name="relu_both", tag="both", align_bytes=64)
         last_relu_b = keep.tile([P, HALF, PACK], F32, name="last_relu_b", align_bytes=64)
-        opening = (slice(0, OPENING), slice(OPENING, CHUNK))
-        for v in opening:
+        halves = (slice(0, HALF), slice(HALF, CHUNK))
+        for v in halves:
             nc.scalar.activation(upper_relu_b[:, v, :], upper_b[:, v, :], ACT.Relu)
         nc.scalar.activation(relu_both[:], mixed[0], ACT.Relu)
         nc.scalar.activation(last_relu_b[:], mixed[1][:, HALF:, :], ACT.Relu)
@@ -156,15 +154,16 @@ def tile_picked_haar_relu_p_kernel(tc, x_words, x_scales, w1, w2, w3, offs, out)
         def band(dst, a_in_bank, relu_b, op):
             nc.vector.scalar_tensor_tensor(dst, a_in_bank, 0.0, relu_b, ALU.max, op)
 
-        def quantized_band(values, name):
-            return quantized(values[:].rearrange("p v t -> p (v t)"), CHUNK, name)
+        def quantized_band(values, name, tag=""):
+            return quantized(values[:].rearrange("p v t -> p (v t)"), CHUNK, name, tag)
 
         upper_low = keep.tile([P, CHUNK, PACK], BF16, name="upper_low", tag="band", align_bytes=64)
         upper_high = keep.tile([P, CHUNK, PACK], BF16, name="upper_high", align_bytes=64)
-        for v in opening:
+        for v in halves:
             band(upper_low[:, v, :], upper_a[:, v, :], upper_relu_b[:, v, :], ALU.add)
-            band(upper_high[:, v, :], upper_a[:, v, :], upper_relu_b[:, v, :], ALU.subtract)
-        upper_q = (quantized_band(upper_low, "upper_low"), quantized_band(upper_high, "upper_high"))
+        band(upper_high[:, :HALF, :], upper_a[:, :HALF, :], upper_relu_b[:, :HALF, :], ALU.subtract)
+        upper_low_q = quantized_band(upper_low, "upper_low")
+        band(upper_high[:, HALF:, :], upper_a[:, HALF:, :], upper_relu_b[:, HALF:, :], ALU.subtract)
 
         lower_low = keep.tile([P, CHUNK, PACK], BF16, name="lower_low", align_bytes=64)
         lower_high = keep.tile([P, CHUNK, PACK], BF16, name="lower_high", tag="band", align_bytes=64)
@@ -172,23 +171,21 @@ def tile_picked_haar_relu_p_kernel(tc, x_words, x_scales, w1, w2, w3, offs, out)
         band(lower_low[:, :HALF, :], mixed[0][:, :HALF, :], relu_both[:, HALF:, :], ALU.add)
         band(lower_low[:, HALF:, :], mixed[1][:, :HALF, :], last_relu_b[:], ALU.add)
         band(lower_high[:, HALF:, :], mixed[1][:, :HALF, :], last_relu_b[:], ALU.subtract)
+        upper_q = (upper_low_q, quantized_band(upper_high, "upper_high", "both"))
         lower_q = (quantized_band(lower_low, "lower_low"), quantized_band(lower_high, "lower_high"))
 
         for first, moving in ((CHUNK, upper_q), (0, lower_q)):
             acc = psum.tile([P, CHUNK], F32, name=f"acc{first}")
-            for i, (codes, scales) in enumerate((w2_q, w3_q)):
+            for i in range(2):
                 nc.tensor.matmul_mx(
                     out=acc[:],
-                    lhsT=codes[:].bitcast(FP8X4),
-                    lhsT_scale=scales[:],
+                    lhsT=w23_codes[:, i * N : (i + 1) * N].bitcast(FP8X4),
+                    lhsT_scale=w23_bytes[:, i * N : (i + 1) * N],
                     rhs=moving[i][0][:].bitcast(FP8X4),
                     rhs_scale=moving[i][1][:],
                     start=(i == 0),
                     stop=(i == 1),
                 )
             result = keep.tile([P, CHUNK], F32, name=f"result{first}")
-            if first:
-                nc.scalar.activation(result[:], acc[:], ACT.Copy, scale=0.5)
-            else:
-                nc.vector.tensor_scalar_mul(result[:], acc[:], 0.5)
+            nc.scalar.activation(result[:], acc[:], ACT.Copy, scale=0.5)
             nc.sync.dma_start(out[:, first : first + CHUNK], result[:])

@@ -21,6 +21,7 @@ HALF_M = P // 2
 CHUNK = 128
 LIST_ROWS = 16
 HALF = CHUNK // 2
+GPSIMD_PAIRS = 48
 WORDS_BYTES = 4 * CHUNK
 
 
@@ -142,13 +143,14 @@ def tile_picked_haar_relu_p_kernel(tc, x_words, x_scales, w1, w2, w3, offs, out)
         gpsimd_cast(w23_grouped[:, 1, N // 2 :, :], w23_raw[1][:, :, N // 2 :].rearrange("p j n -> p n j"))
         w23_codes, w23_bytes = quantized(w23_grouped[:].rearrange("p i n j -> p (i n j)"), 2 * N, "w23")
 
-        upper_relu_b = keep.tile([P, CHUNK, PACK], F32, name="upper_relu_b", align_bytes=64)
+        upper_relu_b = [keep.tile([P, HALF, PACK], F32, name=f"upper_relu_b{h}", tag=f"relu_b{h}", align_bytes=64) for h in range(2)]
         relu_both = keep.tile([P, CHUNK, PACK], F32, name="relu_both", tag="both", align_bytes=64)
         last_relu_b = keep.tile([P, HALF, PACK], F32, name="last_relu_b", align_bytes=64)
         halves = (slice(0, HALF), slice(HALF, CHUNK))
-        for v in halves:
-            nc.scalar.activation(upper_relu_b[:, v, :], upper_b[:, v, :], ACT.Relu)
-        nc.scalar.activation(relu_both[:], mixed[0], ACT.Relu)
+        for h, v in enumerate(halves):
+            nc.scalar.activation(upper_relu_b[h][:], upper_b[:, v, :], ACT.Relu)
+        for v in (slice(0, GPSIMD_PAIRS), slice(HALF, CHUNK)):
+            nc.scalar.activation(relu_both[:, v, :], mixed[0][:, v, :], ACT.Relu)
         nc.scalar.activation(last_relu_b[:], mixed[1][:, HALF:, :], ACT.Relu)
 
         def band(dst, a_in_bank, relu_b, op):
@@ -157,18 +159,21 @@ def tile_picked_haar_relu_p_kernel(tc, x_words, x_scales, w1, w2, w3, offs, out)
         def quantized_band(values, name, tag=""):
             return quantized(values[:].rearrange("p v t -> p (v t)"), CHUNK, name, tag)
 
-        upper_low = keep.tile([P, CHUNK, PACK], BF16, name="upper_low", tag="band", align_bytes=64)
+        upper_low = keep.tile([P, CHUNK, PACK], BF16, name="upper_low", align_bytes=64)
         upper_high = keep.tile([P, CHUNK, PACK], BF16, name="upper_high", align_bytes=64)
-        for v in halves:
-            band(upper_low[:, v, :], upper_a[:, v, :], upper_relu_b[:, v, :], ALU.add)
-        band(upper_high[:, :HALF, :], upper_a[:, :HALF, :], upper_relu_b[:, :HALF, :], ALU.subtract)
+        for h, v in enumerate(halves):
+            band(upper_low[:, v, :], upper_a[:, v, :], upper_relu_b[h][:], ALU.add)
+        band(upper_high[:, :HALF, :], upper_a[:, :HALF, :], upper_relu_b[0][:], ALU.subtract)
         upper_low_q = quantized_band(upper_low, "upper_low")
-        band(upper_high[:, HALF:, :], upper_a[:, HALF:, :], upper_relu_b[:, HALF:, :], ALU.subtract)
+        band(upper_high[:, HALF:, :], upper_a[:, HALF:, :], upper_relu_b[1][:], ALU.subtract)
 
         lower_low = keep.tile([P, CHUNK, PACK], BF16, name="lower_low", align_bytes=64)
-        lower_high = keep.tile([P, CHUNK, PACK], BF16, name="lower_high", tag="band", align_bytes=64)
-        nc.gpsimd.tensor_tensor(lower_high[:, :HALF, :], relu_both[:, :HALF, :], relu_both[:, HALF:, :], ALU.subtract)
+        lower_high = keep.tile([P, CHUNK, PACK], BF16, name="lower_high", tag="relu_b0", align_bytes=64)
+        nc.gpsimd.tensor_tensor(
+            lower_high[:, :GPSIMD_PAIRS, :], relu_both[:, :GPSIMD_PAIRS, :], relu_both[:, HALF : HALF + GPSIMD_PAIRS, :], ALU.subtract
+        )
         band(lower_low[:, :HALF, :], mixed[0][:, :HALF, :], relu_both[:, HALF:, :], ALU.add)
+        band(lower_high[:, GPSIMD_PAIRS:HALF, :], mixed[0][:, GPSIMD_PAIRS:HALF, :], relu_both[:, HALF + GPSIMD_PAIRS :, :], ALU.subtract)
         band(lower_low[:, HALF:, :], mixed[1][:, :HALF, :], last_relu_b[:], ALU.add)
         band(lower_high[:, HALF:, :], mixed[1][:, :HALF, :], last_relu_b[:], ALU.subtract)
         upper_q = (upper_low_q, quantized_band(upper_high, "upper_high", "both"))

@@ -21,7 +21,7 @@ HALF_M = P // 2
 CHUNK = 128
 LIST_ROWS = 16
 HALF = CHUNK // 2
-GPSIMD_PAIRS = 48
+GPSIMD_PAIRS = 56
 WORDS_BYTES = 4 * CHUNK
 
 

@@ -33,16 +33,17 @@ def tile_picked_haar_relu_p_kernel(tc, x_words, x_scales, w1, w2, w3, offs, out)
         psum = ctx.enter_context(tc.psum_pool(name="psum", bufs=1))
 
         byte_table = keep.tile([P, T], U8, name="byte_table", align_bytes=64)
-        nc.gpsimd.memset(byte_table[:].bitcast(I32), 0)
-        staged = keep.tile([P, T], U8, name="staged", align_bytes=64)
-        for q in range(4):
-            queue = nc.sync if q < 2 else nc.scalar
-            queue.dma_start(staged[32 * q : 32 * q + 4, :].bitcast(I32), x_scales[0, 4 * q : 4 * q + 4, :].bitcast(I32))
+        nc.vector.memset(byte_table[:].bitcast(I32), 0)
         offsets = keep.tile([P, S // LIST_ROWS], U16, name="offsets")
         nc.sync.dma_start(offsets[:], offs)
         w1_run = w1.rearrange("(p j) c -> p (j c)", j=PACK)
         w1_front = shared.tile([P, 2, H], F32, name="w1_front", align_bytes=64, offset=0)
-        nc.sync.dma_start(w1_front[:].rearrange("p j c -> p (j c)"), w1_run[:, 0 : 2 * H])
+        front_run = w1_front[:].rearrange("p j c -> p (j c)")
+        nc.sync.dma_start(front_run[:, 0 : H // 2], w1_run[:, 0 : H // 2])
+        for q in range(4):
+            queue = nc.sync if q < 2 else nc.scalar
+            queue.dma_start(byte_table[32 * q : 32 * q + 4, :].bitcast(I32), x_scales[0, 4 * q : 4 * q + 4, :].bitcast(I32))
+        nc.sync.dma_start(front_run[:, H // 2 :], w1_run[:, H // 2 : 2 * H])
         w1_back = keep.tile([P, 2, H], F32, name="w1_back", align_bytes=64)
         back_run = w1_back[:].rearrange("p j c -> p (j c)")
         cut = H + H // 2
@@ -57,9 +58,6 @@ def tile_picked_haar_relu_p_kernel(tc, x_words, x_scales, w1, w2, w3, offs, out)
         def listed(first, count):
             return offsets[:, first // LIST_ROWS : (first + count) // LIST_ROWS]
 
-        for q in range(4):
-            rows = slice(32 * q, 32 * q + 4)
-            nc.vector.tensor_copy(byte_table[rows, :].bitcast(I32), staged[rows, :].bitcast(I32))
         x_bytes = keep.tile([P, S], U8, name="x_bytes", align_bytes=64)
         nc.vector.tensor_copy(x_bytes[:], byte_table[:].indirect(offsets[:]))
 
@@ -75,8 +73,9 @@ def tile_picked_haar_relu_p_kernel(tc, x_words, x_scales, w1, w2, w3, offs, out)
         def gpsimd_cast(dst, src):
             nc.gpsimd.tensor_scalar(dst, src, 1.0, 0.0, ALU.mult, ALU.add)
 
-        for pair, copy in enumerate((nc.scalar.copy, gpsimd_cast)):
-            deal_w1(copy, w1_front, 0, pair, slice(0, P))
+        for cols in (slice(HALF_M, P), slice(0, HALF_M)):
+            deal_w1(nc.scalar.copy, w1_front, 0, 0, cols)
+        deal_w1(gpsimd_cast, w1_front, 0, 1, slice(0, P))
         for h in range(2):
             for pair, copy in enumerate((nc.vector.tensor_copy, nc.scalar.copy)):
                 deal_w1(copy, w1_back, 2, pair, slice(h * HALF_M, (h + 1) * HALF_M))

@@ -18,6 +18,7 @@ ACT = mybir.ActivationFunctionType
 P = 128
 PACK = 4
 HALF_M = P // 2
+SCALAR_M = 96
 CHUNK = 128
 LIST_ROWS = 16
 HALF = CHUNK // 2
@@ -34,16 +35,16 @@ def tile_picked_haar_relu_p_kernel(tc, x_words, x_scales, w1, w2, w3, offs, out)
 
         byte_table = keep.tile([P, T], U8, name="byte_table", align_bytes=64)
         nc.vector.memset(byte_table[:].bitcast(I32), 0)
-        offsets = keep.tile([P, S // LIST_ROWS], U16, name="offsets")
-        nc.sync.dma_start(offsets[:], offs)
+        w1_rows = w1.rearrange("(p j) c -> p j c", j=PACK)
         w1_run = w1.rearrange("(p j) c -> p (j c)", j=PACK)
         w1_front = shared.tile([P, 2, H], F32, name="w1_front", align_bytes=64, offset=0)
-        front_run = w1_front[:].rearrange("p j c -> p (j c)")
-        nc.sync.dma_start(front_run[:, 0 : H // 2], w1_run[:, 0 : H // 2])
+        nc.sync.dma_start(w1_front[:, :, 0 : H // 2], w1_rows[:, 0:2, 0 : H // 2])
+        offsets = keep.tile([P, S // LIST_ROWS], U16, name="offsets")
+        nc.sync.dma_start(offsets[:], offs)
         for q in range(4):
             queue = nc.sync if q < 2 else nc.scalar
             queue.dma_start(byte_table[32 * q : 32 * q + 4, :].bitcast(I32), x_scales[0, 4 * q : 4 * q + 4, :].bitcast(I32))
-        nc.sync.dma_start(front_run[:, H // 2 :], w1_run[:, H // 2 : 2 * H])
+        nc.sync.dma_start(w1_front[:, :, H // 2 :], w1_rows[:, 0:2, H // 2 :])
         w1_back = keep.tile([P, 2, H], F32, name="w1_back", align_bytes=64)
         back_run = w1_back[:].rearrange("p j c -> p (j c)")
         cut = H + H // 2
@@ -58,44 +59,46 @@ def tile_picked_haar_relu_p_kernel(tc, x_words, x_scales, w1, w2, w3, offs, out)
         def listed(first, count):
             return offsets[:, first // LIST_ROWS : (first + count) // LIST_ROWS]
 
-        x_bytes = keep.tile([P, S], U8, name="x_bytes", align_bytes=64)
-        nc.vector.tensor_copy(x_bytes[:], byte_table[:].indirect(offsets[:]))
+        x_bytes = keep.tile([P, V + CHUNK], U8, name="x_bytes", align_bytes=64)
+        nc.vector.tensor_copy(x_bytes[:], byte_table[:].indirect(listed(0, V + CHUNK)))
+        upper_b_bytes = keep.tile([P, CHUNK], U8, name="upper_b_bytes", align_bytes=64)
+        nc.vector.tensor_copy(upper_b_bytes[:], byte_table[:].indirect(listed(V + CHUNK, CHUNK)))
 
         w1_codes = keep.tile([P, PACK, P], U32, name="w1_codes", align_bytes=64)
         w1_bytes = keep.tile([P, PACK, P], U8, name="w1_bytes", align_bytes=64)
-        grouped = keep.tile([P, PACK, P, PACK], BF16, name="w1_grouped", align_bytes=64)
+        grouped = [keep.tile([P, 2, P, PACK], BF16, name=f"w1_grouped{pair}", align_bytes=64) for pair in range(2)]
 
         def deal_w1(copy, raw, j0, pair, cols):
             src = raw[:, :, PACK * cols.start : PACK * cols.stop].rearrange("p j (m t) -> p m t j", t=PACK)
-            dst = grouped[:, 2 * pair : 2 * pair + 2, cols, j0 : j0 + 2].rearrange("p t m j -> p m t j")
+            dst = grouped[pair][:, :, cols, j0 : j0 + 2].rearrange("p t m j -> p m t j")
             copy(dst, src[:, :, 2 * pair : 2 * pair + 2, :])
 
         def gpsimd_cast(dst, src):
             nc.gpsimd.tensor_scalar(dst, src, 1.0, 0.0, ALU.mult, ALU.add)
 
-        for cols in (slice(HALF_M, P), slice(0, HALF_M)):
-            deal_w1(nc.scalar.copy, w1_front, 0, 0, cols)
-        deal_w1(gpsimd_cast, w1_front, 0, 1, slice(0, P))
+        for pair, copy in enumerate((nc.scalar.copy, gpsimd_cast)):
+            deal_w1(copy, w1_front, 0, pair, slice(0, HALF_M))
+        deal_w1(nc.scalar.copy, w1_front, 0, 0, slice(HALF_M, P))
+        deal_w1(gpsimd_cast, w1_front, 0, 1, slice(HALF_M, SCALAR_M))
+        deal_w1(nc.scalar.copy, w1_front, 0, 1, slice(SCALAR_M, P))
         for h in range(2):
-            for pair, copy in enumerate((nc.vector.tensor_copy, nc.scalar.copy)):
-                deal_w1(copy, w1_back, 2, pair, slice(h * HALF_M, (h + 1) * HALF_M))
+            deal_w1(nc.vector.tensor_copy, w1_back, 2, 0, slice(h * HALF_M, (h + 1) * HALF_M))
+        for copy, cols in ((nc.scalar.copy, slice(0, HALF_M)), (nc.scalar.copy, slice(HALF_M, SCALAR_M)), (nc.vector.tensor_copy, slice(SCALAR_M, P))):
+            deal_w1(copy, w1_back, 2, 1, cols)
 
-        def quantize_w1(h, slots):
-            cols = slice(h * HALF_M, (h + 1) * HALF_M)
-            for t in slots:
-                nc.vector.quantize_mx(
-                    out=w1_codes[:, t, cols].bitcast(FP8X4),
-                    scales=w1_bytes[:, t, cols],
-                    in_=grouped[:, t, cols, :].rearrange("p m j -> p (m j)"),
-                )
 
         mixed_bytes = keep.tile([P, 2, 2, HALF], U8, name="mixed_bytes", align_bytes=64)
         nc.vector.tensor_copy(
             mixed_bytes[:].bitcast(I32),
-            x_bytes[:].bitcast(I32).rearrange("p (d c h w) -> p c h d w", d=2, c=2, h=2)[:, 0],
+            x_bytes[:].bitcast(I32).rearrange("p (r h w) -> p h r w", r=3, h=2)[:, :, 0:3:2, :],
         )
-        for h in range(2):
-            quantize_w1(h, range(PACK))
+        for pair in range(2):
+            slots = slice(2 * pair, 2 * pair + 2)
+            nc.vector.quantize_mx(
+                out=w1_codes[:, slots, :].rearrange("p t m -> p (t m)").bitcast(FP8X4),
+                scales=w1_bytes[:, slots, :].rearrange("p t m -> p (t m)"),
+                in_=grouped[pair][:].rearrange("p t m j -> p (t m j)"),
+            )
 
         plain_words = []
         for n, first in enumerate((V + CHUNK, CHUNK)):
@@ -120,7 +123,7 @@ def tile_picked_haar_relu_p_kernel(tc, x_words, x_scales, w1, w2, w3, offs, out)
                 )
             return bank[:].rearrange("p t v -> p v t")
 
-        upper_b = first_product("upper_b", plain_words[0][:], x_bytes[:, V + CHUNK :])
+        upper_b = first_product("upper_b", plain_words[0][:], upper_b_bytes[:])
         upper_a = first_product("upper_a", plain_words[1][:], x_bytes[:, CHUNK:V])
         mixed = [
             first_product(f"mixed{h}", mixed_words[:, h].rearrange("p d v -> p (d v)"), mixed_bytes[:, h].rearrange("p d v -> p (d v)"))

from contextlib import ExitStack

import concourse.mybir as mybir

K, T, S, V, H, N = 512, 1024, 512, 256, 512, 128
FLOPS = 2 * K * H * S + 2 * 2 * H * N * V

F32 = mybir.dt.float32
BF16 = mybir.dt.bfloat16
I32 = mybir.dt.int32
U32 = mybir.dt.uint32
U16 = mybir.dt.uint16
U8 = mybir.dt.uint8
FP8X4 = mybir.dt.float8_e4m3fn_x4
ALU = mybir.AluOpType
ACT = mybir.ActivationFunctionType

P = 128
PACK = 4
HALF_M = P // 2
SCALAR_M = 96
CHUNK = 128
LIST_ROWS = 16
HALF = CHUNK // 2
GPSIMD_PAIRS = 56
WORDS_BYTES = 4 * CHUNK


def tile_picked_haar_relu_p_kernel(tc, x_words, x_scales, w1, w2, w3, offs, out):
    nc = tc.nc
    with ExitStack() as ctx:
        keep = ctx.enter_context(tc.tile_pool(name="keep", bufs=1))
        shared = ctx.enter_context(tc.tile_pool(name="shared", bufs=1))
        psum = ctx.enter_context(tc.psum_pool(name="psum", bufs=1))

        byte_table = keep.tile([P, T], U8, name="byte_table", align_bytes=64)
        nc.vector.memset(byte_table[:].bitcast(I32), 0)
        w1_rows = w1.rearrange("(p j) c -> p j c", j=PACK)
        w1_run = w1.rearrange("(p j) c -> p (j c)", j=PACK)
        w1_front = shared.tile([P, 2, H], F32, name="w1_front", align_bytes=64, offset=0)
        nc.sync.dma_start(w1_front[:, :, 0 : H // 2], w1_rows[:, 0:2, 0 : H // 2])
        offsets = keep.tile([P, S // LIST_ROWS], U16, name="offsets")
        nc.sync.dma_start(offsets[:], offs)
        for q in range(4):
            queue = nc.sync if q < 2 else nc.scalar
            queue.dma_start(byte_table[32 * q : 32 * q + 4, :].bitcast(I32), x_scales[0, 4 * q : 4 * q + 4, :].bitcast(I32))
        nc.sync.dma_start(w1_front[:, :, H // 2 :], w1_rows[:, 0:2, H // 2 :])
        w1_back = keep.tile([P, 2, H], F32, name="w1_back", align_bytes=64)
        back_run = w1_back[:].rearrange("p j c -> p (j c)")
        cut = H + H // 2
        nc.sync.dma_start(back_run[:, 0:cut], w1_run[:, 2 * H : 2 * H + cut])
        nc.sync.dma_start(back_run[:, cut:], w1_run[:, 2 * H + cut :])
        word_table = keep.tile([P, T], U32, name="word_table", align_bytes=64)
        nc.sync.dma_start(word_table[:].bitcast(I32), x_words[0].rearrange("p n t -> p (n t)").bitcast(I32))
        w23_raw = [keep.tile([P, PACK, N], F32, name=f"w23_raw{i}") for i in range(2)]
        for i, w in enumerate((w2, w3)):
            nc.sync.dma_start(w23_raw[i][:], w.rearrange("(p j) n -> p j n", j=PACK))

        def listed(first, count):
            return offsets[:, first // LIST_ROWS : (first + count) // LIST_ROWS]

        x_bytes = keep.tile([P, V + CHUNK], U8, name="x_bytes", align_bytes=64)
        nc.vector.tensor_copy(x_bytes[:], byte_table[:].indirect(listed(0, V + CHUNK)))
        upper_b_bytes = keep.tile([P, CHUNK], U8, name="upper_b_bytes", align_bytes=64)
        nc.vector.tensor_copy(upper_b_bytes[:], byte_table[:].indirect(listed(V + CHUNK, CHUNK)))

        w1_codes = keep.tile([P, PACK, P], U32, name="w1_codes", align_bytes=64)
        w1_bytes = keep.tile([P, PACK, P], U8, name="w1_bytes", align_bytes=64)
        grouped = [keep.tile([P, 2, P, PACK], BF16, name=f"w1_grouped{pair}", align_bytes=64) for pair in range(2)]

        def deal_w1(copy, raw, j0, pair, cols):
            src = raw[:, :, PACK * cols.start : PACK * cols.stop].rearrange("p j (m t) -> p m t j", t=PACK)
            dst = grouped[pair][:, :, cols, j0 : j0 + 2].rearrange("p t m j -> p m t j")
            copy(dst, src[:, :, 2 * pair : 2 * pair + 2, :])

        def gpsimd_cast(dst, src):
            nc.gpsimd.tensor_scalar(dst, src, 1.0, 0.0, ALU.mult, ALU.add)

        for pair, copy in enumerate((nc.scalar.copy, gpsimd_cast)):
            deal_w1(copy, w1_front, 0, pair, slice(0, HALF_M))
        deal_w1(nc.scalar.copy, w1_front, 0, 0, slice(HALF_M, P))
        deal_w1(gpsimd_cast, w1_front, 0, 1, slice(HALF_M, SCALAR_M))
        deal_w1(nc.scalar.copy, w1_front, 0, 1, slice(SCALAR_M, P))
        for h in range(2):
            deal_w1(nc.vector.tensor_copy, w1_back, 2, 0, slice(h * HALF_M, (h + 1) * HALF_M))
        for copy, cols in ((nc.scalar.copy, slice(0, HALF_M)), (nc.scalar.copy, slice(HALF_M, SCALAR_M)), (nc.vector.tensor_copy, slice(SCALAR_M, P))):
            deal_w1(copy, w1_back, 2, 1, cols)


        mixed_bytes = keep.tile([P, 2, 2, HALF], U8, name="mixed_bytes", align_bytes=64)
        nc.vector.tensor_copy(
            mixed_bytes[:].bitcast(I32),
            x_bytes[:].bitcast(I32).rearrange("p (r h w) -> p h r w", r=3, h=2)[:, :, 0:3:2, :],
        )
        for pair in range(2):
            slots = slice(2 * pair, 2 * pair + 2)
            nc.vector.quantize_mx(
                out=w1_codes[:, slots, :].rearrange("p t m -> p (t m)").bitcast(FP8X4),
                scales=w1_bytes[:, slots, :].rearrange("p t m -> p (t m)"),
                in_=grouped[pair][:].rearrange("p t m j -> p (t m j)"),
            )

        plain_words = []
        for n, first in enumerate((V + CHUNK, CHUNK)):
            picked = shared.tile([P, CHUNK], U32, name=f"words{n}", align_bytes=64, offset=n * WORDS_BYTES)
            nc.vector.tensor_copy(picked[:], word_table[:].indirect(listed(first, CHUNK)))
            plain_words.append(picked)
        mixed_words = shared.tile([P, 2, 2, HALF], U32, name="mixed_words", align_bytes=64, offset=2 * WORDS_BYTES)
        for d in range(2):
            nc.vector.tensor_copy(mixed_words[:, :, d, :], word_table[:].indirect(listed(d * V, CHUNK)))

        def first_product(name, words, scales):
            bank = psum.tile([P, PACK, CHUNK], F32, name=name)
            for t in range(PACK):
                nc.tensor.matmul_mx(
                    out=bank[:, t, :],
                    lhsT=w1_codes[:, t, :].bitcast(FP8X4),
                    lhsT_scale=w1_bytes[:, t, :],
                    rhs=words.bitcast(FP8X4),
                    rhs_scale=scales,
                    start=True,
                    stop=True,
                )
            return bank[:].rearrange("p t v -> p v t")

        upper_b = first_product("upper_b", plain_words[0][:], upper_b_bytes[:])
        upper_a = first_product("upper_a", plain_words[1][:], x_bytes[:, CHUNK:V])
        mixed = [
            first_product(f"mixed{h}", mixed_words[:, h].rearrange("p d v -> p (d v)"), mixed_bytes[:, h].rearrange("p d v -> p (d v)"))
            for h in range(2)
        ]

        def quantized(values, width, name, tag=""):
            codes = keep.tile([P, width], U32, name=f"{name}_codes", tag=tag, align_bytes=64)
            scales = keep.tile([P, width], U8, name=f"{name}_bytes", align_bytes=64)
            nc.vector.quantize_mx(out=codes[:].bitcast(FP8X4), scales=scales[:], in_=values)
            return codes, scales

        w23_grouped = shared.tile([P, 2, N, PACK], BF16, name="w23_grouped", align_bytes=64, offset=4 * WORDS_BYTES)
        for i, cols in ((0, slice(0, N)), (1, slice(0, N // 2))):
            nc.scalar.copy(
                w23_grouped[:, i, cols, :].rearrange("p (n i) j -> p n j i", i=4),
                w23_raw[i][:, :, cols].rearrange("p j (n i) -> p n j i", i=4),
            )
        gpsimd_cast(w23_grouped[:, 1, N // 2 :, :], w23_raw[1][:, :, N // 2 :].rearrange("p j n -> p n j"))
        w23_codes, w23_bytes = quantized(w23_grouped[:].rearrange("p i n j -> p (i n j)"), 2 * N, "w23")

        upper_relu_b = [keep.tile([P, HALF, PACK], F32, name=f"upper_relu_b{h}", tag=f"relu_b{h}", align_bytes=64) for h in range(2)]
        relu_both = keep.tile([P, CHUNK, PACK], F32, name="relu_both", tag="both", align_bytes=64)
        last_relu_b = keep.tile([P, HALF, PACK], F32, name="last_relu_b", align_bytes=64)
        halves = (slice(0, HALF), slice(HALF, CHUNK))
        for h, v in enumerate(halves):
            nc.scalar.activation(upper_relu_b[h][:], upper_b[:, v, :], ACT.Relu)
        for v in (slice(0, GPSIMD_PAIRS), slice(HALF, CHUNK)):
            nc.scalar.activation(relu_both[:, v, :], mixed[0][:, v, :], ACT.Relu)
        nc.scalar.activation(last_relu_b[:], mixed[1][:, HALF:, :], ACT.Relu)

        def band(dst, a_in_bank, relu_b, op):
            nc.vector.scalar_tensor_tensor(dst, a_in_bank, 0.0, relu_b, ALU.max, op)

        def quantized_band(values, name, tag=""):
            return quantized(values[:].rearrange("p v t -> p (v t)"), CHUNK, name, tag)

        upper_low = keep.tile([P, CHUNK, PACK], BF16, name="upper_low", align_bytes=64)
        upper_high = keep.tile([P, CHUNK, PACK], BF16, name="upper_high", align_bytes=64)
        for h, v in enumerate(halves):
            band(upper_low[:, v, :], upper_a[:, v, :], upper_relu_b[h][:], ALU.add)
        band(upper_high[:, :HALF, :], upper_a[:, :HALF, :], upper_relu_b[0][:], ALU.subtract)
        upper_low_q = quantized_band(upper_low, "upper_low")
        band(upper_high[:, HALF:, :], upper_a[:, HALF:, :], upper_relu_b[1][:], ALU.subtract)

        lower_low = keep.tile([P, CHUNK, PACK], BF16, name="lower_low", align_bytes=64)
        lower_high = keep.tile([P, CHUNK, PACK], BF16, name="lower_high", tag="relu_b0", align_bytes=64)
        nc.gpsimd.tensor_tensor(
            lower_high[:, :GPSIMD_PAIRS, :], relu_both[:, :GPSIMD_PAIRS, :], relu_both[:, HALF : HALF + GPSIMD_PAIRS, :], ALU.subtract
        )
        band(lower_low[:, :HALF, :], mixed[0][:, :HALF, :], relu_both[:, HALF:, :], ALU.add)
        band(lower_high[:, GPSIMD_PAIRS:HALF, :], mixed[0][:, GPSIMD_PAIRS:HALF, :], relu_both[:, HALF + GPSIMD_PAIRS :, :], ALU.subtract)
        band(lower_low[:, HALF:, :], mixed[1][:, :HALF, :], last_relu_b[:], ALU.add)
        band(lower_high[:, HALF:, :], mixed[1][:, :HALF, :], last_relu_b[:], ALU.subtract)
        upper_q = (upper_low_q, quantized_band(upper_high, "upper_high", "both"))
        lower_q = (quantized_band(lower_low, "lower_low"), quantized_band(lower_high, "lower_high"))

        for first, moving in ((CHUNK, upper_q), (0, lower_q)):
            acc = psum.tile([P, CHUNK], F32, name=f"acc{first}")
            for i in range(2):
                nc.tensor.matmul_mx(
                    out=acc[:],
                    lhsT=w23_codes[:, i * N : (i + 1) * N].bitcast(FP8X4),
                    lhsT_scale=w23_bytes[:, i * N : (i + 1) * N],
                    rhs=moving[i][0][:].bitcast(FP8X4),
                    rhs_scale=moving[i][1][:],
                    start=(i == 0),
                    stop=(i == 1),
                )
            result = keep.tile([P, CHUNK], F32, name=f"result{first}")
            nc.scalar.activation(result[:], acc[:], ACT.Copy, scale=0.5)
            nc.sync.dma_start(out[:, first : first + CHUNK], result[:])
